import numpy as np, ml_dtypes
CORES = [35,38,43,46]
N = 4
BF = ml_dtypes.bfloat16
def gentries(a):
    return np.ascontiguousarray(a.reshape(8, 16, -1).transpose(0, 2, 1)).reshape(8, -1)
def gtable(e):
    e = np.asarray(e); return np.ascontiguousarray(e.reshape(8, -1, 16).transpose(0, 2, 1)).reshape(128, -1).astype(np.int32)
P, C, CAP, TH, DAYS, BITS = 1024, 4, 384, 1200, 4, 11
W = N * P; M = 2 ** BITS; B0 = TH // 16; DEC = 8; STEP = 77
def parts(rng):
    x = (rng.random((N, 8, 16, P)) * B0 * rng.random((N, 8, 1, P))).astype(np.int64); x = np.minimum(x, B0 - 1)
    return x, rng.integers(0, W, (N, 8, C * P)), rng.integers(0, M, (N, 8, C * P)), rng.integers(0, 256, (N, 8, P))
def even(rng):
    u = rng.integers(-B0, B0 + 1, (N, 8, 8, P)); u[:, :, 0] = np.abs(u[:, :, 0])
    return np.concatenate([B0 + u, B0 - u], axis=2)
def sick(rng):
    e = even(rng)
    return np.minimum(e + ((256 - e) * rng.random((N, 8, 1, P)) * rng.random(e.shape)).astype(np.int64), 255)
def lean(rng):
    n = rng.integers(-(-TH // 255), 9, (N, 8, 1, P)); s = rng.integers(0, 16, (N, 8, 1, P)); lo = -(-TH // n)
    on = (np.arange(16)[:, None] - s) % 16 < n
    return np.where(on, np.minimum(lo + ((256 - lo) * rng.random((N, 8, 16, P))).astype(np.int64), 255), 0)
def mark(rng, x, share):
    return np.where(rng.random((N, 8, 1, P)) < share, sick(rng), x)
def pack(x, nb, dice, res):
    return {"x0": np.ascontiguousarray(x.reshape(N, 128, P)).astype(np.int32), "nb": np.stack([gtable(v) for v in nb]), "dice": np.stack([gtable(v) for v in dice]), "res": np.ascontiguousarray(res).astype(np.int32)}
def setup_inputs(rng):
    x, nb, dice, res = parts(rng); share = rng.choice(np.array([0.04, 0.1, 0.2, 0.45]), (N, 8, 1, 1))
    return pack(mark(rng, x, share), nb, dice, res)
def setup_inputs_room(rng):
    x, nb, dice, res = parts(rng); m = np.zeros((N, 8, P), bool)
    n = rng.choice(np.array([0, 1, CAP - 1, CAP, CAP + 1, P]), (N, 8))
    n[0] = (CAP, CAP + 1, P, CAP - 1, 1, 0, CAP, CAP + 1)
    n[1] = (0, P, CAP + 1, 1, CAP - 1, CAP, CAP, CAP)
    n[2] = (CAP, CAP + 1, CAP, P, CAP, CAP + 1, CAP, CAP)
    n[3, ::2] = CAP
    j = P - CAP; cnt = W - int(np.sum(np.minimum(n[:, 6], CAP)))
    while -(-j * M // cnt) * cnt >= (j + 1) * M: j += 1; cnt += 1
    n[0, 6] = P - j; d = -(-j * M // cnt)
    for q in range(N):
        for g in range(8):
            o = rng.permutation(P)
            if (q == 0 and g >= 6) or (q == 1 and g == 7): o = np.arange(P)[::-1]
            if (q == 1 and g == 6) or (q == 2 and g == 7): o = np.arange(P)
            if q == 3: o = np.argsort(rng.permutation(16)[np.arange(P) % 16], kind="stable")
            m[q, g, o[:int(n[q, g])]] = True
    x = np.where(m[:, :, None, :], sick(rng), x)
    x[:, 6] = np.where(m[:, 6][:, None, :], even(rng)[:, 6], x[:, 6]); res[:, 6] = 255
    dice[:, 6] = np.where(rng.random((N, C * P)) < 0.1, d, dice[:, 6])
    return pack(x, nb, dice, res)
def setup_inputs_ties(rng):
    x, nb, dice, res = parts(rng)
    x = np.where(rng.random((N, 8, 1, P)) < 0.2, rng.choice(np.array([0, 7, 8, 9]), x.shape), x)
    x = mark(rng, x, 0.06); e = even(rng); e[:, :, 0] += rng.integers(-1, 2, (N, 8, P))
    x = np.where(rng.random((N, 8, 1, P)) < 0.35, e, x)
    x = np.where(rng.random((N, 8, 1, P)) < 0.08, lean(rng), x)
    res = np.where(rng.random(res.shape) < 0.7, rng.choice(np.array([0, 1, 7, 8, 9, 255]), res.shape), res)
    return pack(x, nb, dice, res)
def setup_inputs_ends(rng):
    x, nb, dice, res = parts(rng); x = mark(rng, x, 0.15); s = sick(rng)
    x[..., 0] = s[..., 0]; x[..., P - 1] = s[..., P - 1]
    nb[:, 1::2] = np.tile(nb[:, 1::2, :P], (1, 1, C))
    nb[:, 2] = rng.choice(np.array([0, P - 1, W - P, W - 1]), (N, C * P))
    nb[:, 4] = P * np.arange(N)[:, None] + rng.integers(0, P, (N, C * P))
    me = P * np.arange(N)[:, None] + np.tile(np.arange(P), C)[None, :]
    nb[:, 6] = np.where(rng.random((N, C * P)) < 0.5, me, nb[:, 6])
    dice = np.where(rng.random(dice.shape) < 0.8, rng.choice(np.array([0, 1, M - 1, M - 2, M - STEP, M - STEP - 1, M - 2 * STEP, M // 2]), dice.shape), dice)
    return pack(x, nb, dice, res)
def setup_inputs_cold(rng):
    x, nb, dice, res = parts(rng); share = rng.choice(np.array([0.05, 0.15, 0.3]), (N, 8, 1, 1))
    q = rng.permutation(N); c = rng.permutation(8)
    share[q[0]] = 1.0; share[q[1]] = 0.0; share[:, c[0]] = 0.0; share[:, c[1]] = 1.0; share[:, c[[2, 4, 5]]] = 0.0
    x = mark(rng, x, share); e = even(rng)
    a, v = int(rng.integers(0, N)), int(rng.integers(0, P)); x[a, c[2], :, v] = 255
    late = rng.random((N, 1, P)) < 0.25; last = np.arange(C)[:, None] == C - 1
    nb[:, c[2]] = np.where((last | ~late).reshape(N, C * P), a * P + v, nb[:, c[2]])
    nb[q[1], c[3]] = q[0] * P + rng.integers(0, CAP, C * P)
    h = rng.random((N, 1, P)) < 0.2; stay = rng.random((N, 1, P)) < 0.5; stay[q[2]] = False
    x[:, c[4]] = np.where(h, np.where(stay, 255, e[:, c[4]]), x[:, c[4]]); res[:, c[4]] = 255
    h = rng.random((N, P)) < 0.1; u = np.arange(W).reshape(N, P)
    x[:, c[5]] = np.where(h[:, None, :], rng.integers(min(B0 + DEC * DAYS, 255), 256, (N, 16, P)), x[:, c[5]]); res[:, c[5]] = rng.integers(0, 32, (N, P))
    nb[:, c[5]] = np.where(np.tile(h, (1, C)), rng.choice(u[h], (N, C * P)), rng.choice(u[~h], (N, C * P)))
    return pack(x, nb, dice, res)
def setup_inputs_spread(rng):
    x, nb, dice, res = parts(rng)
    x = np.minimum((np.exp2(8 * rng.random((N, 8, 1, P))) * rng.random((N, 8, 16, P))).astype(np.int64), 255)
    res = np.minimum(np.exp2(8 * rng.random((N, 8, P))).astype(np.int64) - 1, 255)
    nb = np.minimum((W * rng.random((N, 8, C * P)) ** rng.choice(np.array([1, 2, 3]), (N, 8, 1))).astype(np.int64), W - 1)
    dice = np.minimum((M * rng.random((N, 8, C * P)) ** 2).astype(np.int64), M - 1)
    return pack(x, nb, dice, res)
def check_inputs(d):
    bad = []
    for k, hi in (("x0", 255), ("nb", W - 1), ("dice", M - 1), ("res", 255)):
        if np.min(d[k]) < 0 or np.max(d[k]) > hi: bad.append("range of " + k)
    return bad
def reference(x0, nb, dice, res):
    x = x0.astype(np.int64).reshape(N, 8, 16, P); r = res.astype(np.int64).reshape(N, 8, 1, P)
    link = np.stack([gentries(v) for v in nb]).astype(np.int64); dr = np.stack([gentries(v) for v in dice]).astype(np.int64)
    for t in range(DAYS):
        high = (np.add.reduce(x, axis=2) >= TH).astype(np.int64); before = np.add.accumulate(high, axis=2) - high
        ill = (high == 1) & (before < CAP)
        flag = np.ascontiguousarray(ill.transpose(1, 0, 2)).reshape(8, W)
        win = np.ascontiguousarray(np.where(ill[:, :, None, :], x, 0).transpose(1, 2, 0, 3)).reshape(8, 16, W)
        come = []
        for q in range(N):
            come.append(np.maximum.reduce(np.take_along_axis(win, link[q][:, None, :], 2).reshape(8, 16, C, P), axis=2))
        d = (dr + STEP * t) & (M - 1); new = link.copy()
        for g in range(8):
            sl = np.flatnonzero(~flag[g])
            hit = flag[g][link[:, g]] & ~np.tile(ill[:, g], (1, C))
            new[:, g] = np.where(hit, sl[(d[:, g] * len(sl)) >> BITS], link[:, g])
        x = np.maximum(np.maximum(x - DEC, np.stack(come) - r), 0); link = new
    return {"yx": x.reshape(N, 128, P).astype(np.float32), "ynb": np.stack([gtable(v) for v in link]).astype(np.float32)}

@@ -1,0 +1,475 @@
+from concourse.bass import DstId, RemoteDMATransfer
+from concourse.mybir import AluOpType as A, ActivationFunctionType as F, AxisListType as X
+
+DAYS, P, CAP, TH, STEP, M2 = 4, 1024, 384, 1200, 77, 2047
+H = 512
+EPS = 2.0 ** -12
+SH = 8192.0
+LQ = {"00": "V", "10": "S", "20": "S", "30": "S", "01": "S", "11": "S", "21": "S", "31": "S"}
+SQ = {"00": "S", "10": "S", "20": "S", "30": "S", "01": "S", "11": "S", "21": "S", "31": "S"}
+LQL = {"00": "S", "10": "V", "20": "V", "30": "S", "01": "S", "11": "S", "21": "S", "31": "S"}
+SQL = {"00": "S", "10": "S", "20": "S", "30": "V", "01": "S", "11": "V", "21": "V", "31": "S"}
+MQ = "VS"
+FIRST = """T0 a0 F0 T1 num D1 v0 a1 off s0 m0 F1 v1 misc Z0 Z1 s1 Z2 m1 Z3 C0 Z4 D0 Z5 C1 M"""
+DAY = """g00 g10 g20 l10 l20 p0 r0 p1 g11 r1 b0 g30 g01 n0 l11 p2 h00 T0 a0 g21 l21 p3 F0 h01 v0 g31 p4 b1 n1 s0 u0 T1 k31 m0
+ k20 a1 D1 F1 k11 D0 v1 k10 s1 k00 Z0 m1 Z1 Z2 k30 C0 k21 Z3 h1 k01 C1 S0 u1 Z4 K0 Z5 M R0 O0 S1 K1 R1 O1"""
+LAST = """g10 g30 g00 g20 p0 g11 r0 g01 l10 p1 l20 h00 p2 l11 p3 b0 p4 g31 n0 h01 g21 l21 u0 k10 k30 r1 k00 k11 k20 k01 k31 b1
+ h1 u1 k21 n1 K1 S0 K0 S1 R0 R1"""
+
+
+def _sb(dtype, *names, cols, rows=128):
+    return {n: ("sbuf", [rows, cols], dtype) for n in names}
+
+
+SCRATCH = {}
+SCRATCH.update(_sb("int32", "xi", cols=P))
+SCRATCH.update(_sb("int32", "ni", "di", "dtmp", "oi", "dd0", "dd1", "dd2", "dd3", cols=256))
+SCRATCH.update(_sb("int32", "t1", "t2", "t2s", cols=128))
+SCRATCH.update(_sb("int32", "ri", cols=64))
+SCRATCH.update(_sb("int32", "t3", cols=16))
+SCRATCH.update(_sb("int32", "pmi", cols=1))
+SCRATCH.update(_sb("uint16", "off", "offs0", "offs1", cols=256))
+SCRATCH.update(_sb("uint16", "pos16", cols=64))
+SCRATCH.update(_sb("bfloat16", "xa", "xc", "xm", "mm", "dat", cols=P))
+SCRATCH.update(_sb("bfloat16", "raw", "rsl", cols=4 * P))
+SCRATCH.update(_sb("bfloat16", *["win%d" % _t for _t in range(DAYS)], *["sw%d" % _t for _t in range(DAYS)], cols=4 * P))
+SCRATCH.update(_sb("bfloat16", "rneg", "lo", cols=P, rows=8))
+SCRATCH.update(_sb("bfloat16", "er", cols=128, rows=8))
+SCRATCH.update(_sb("bfloat16", "ex", cols=2048))
+SCRATCH.update(_sb("bfloat16", "sg", cols=256))
+SCRATCH.update(_sb("bfloat16", "bp", "cp", cols=144))
+SCRATCH.update(_sb("bfloat16", "mb", "idn", "id2", "id3", "id4", "ineg", "su", "su1", "i2", "su2", cols=128))
+SCRATCH.update(_sb("bfloat16", "high", "ill0", "ill1", "rw", cols=64))
+SCRATCH.update(_sb("float32", "yo", cols=P))
+SCRATCH.update(_sb("float32", "no", "lk", "hh", "nf", cols=256))
+SCRATCH.update(_sb("float32", "pre", "zz", "cum", "ee", "pos", "z64", "vvc", "vv", "sel", cols=64))
+SCRATCH.update(_sb("float32", "cnt", cols=16 * DAYS))
+SCRATCH.update(_sb("float32", "r16", cols=16))
+SCRATCH.update(_sb("float32", "pmf", "ka", "kb", cols=4))
+for _b in ("c0", "c1", "e0", "e1", "ht", "sl", "tc0", "tc1"):
+    SCRATCH[_b] = ("psum", [128, 512], "float32")
+SEMAPHORES = ["pv", "ps", "pp", "pg", "sent"] + ["dm%d" % i for i in range(16)]
+SEMAPHORES += [k + "%d" % t for k in ("al", "ah", "ac", "as") for t in range(DAYS)]
+
+
+def plan(topo, cores, src):
+    far = [d for d in cores if d != src and topo.chip(d) != topo.chip(src)]
+    near = [d for d in cores if d != src and topo.chip(d) == topo.chip(src)]
+    e = {}
+    used = []
+    for n, d in enumerate(far):
+        es = topo.engines(src, d)
+        w = len(es) // len(far)
+        e[d] = es[n * w:(n + 1) * w]
+        used += e[d]
+    for n, d in enumerate(near):
+        es = [x for x in topo.engines(src, d) if x not in used]
+        w = len(es) // len(near)
+        e[d] = es[n * w:(n + 1) * w]
+    return e
+
+
+def rank_program(g, core, T, topo):
+    q = T.rank_of(core)
+    if q is None:
+        return
+    cores = list(T.cores)
+    right = q % 2 == 0
+    eng = {c: plan(topo, cores, c) for c in cores}
+    queue = {"V": g.vector, "S": g.scalar, "P": g.tensor, "G": g, "Y": g.sync}
+    psem = {"V": "pv", "S": "ps", "P": "pp", "G": "pg"}
+    done = {k: 0 for k in queue}
+    known = {k: {} for k in queue}
+    lastw, readers = {}, {}
+    ndma = [0]
+    nsent = [0]
+
+    def sync_to(qn, toks):
+        need = {}
+        for t in toks:
+            if known[qn].get(t[0], 0) < t[1]:
+                if t[1] > need.get(t[0], (0,))[0]:
+                    need[t[0]] = (t[1], t)
+        for s in sorted(need):
+            v, t = need[s]
+            if any(o != s and need[o][1][2].get(s, 0) >= v for o in need):
+                continue
+            queue[qn].wait_ge(T.sem[s], v)
+        for s in need:
+            v, t = need[s]
+            for k2, v2 in t[2].items():
+                if known[qn].get(k2, 0) < v2:
+                    known[qn][k2] = v2
+            if known[qn].get(s, 0) < v:
+                known[qn][s] = v
+
+    def deps(qn, reads, writes, accum):
+        toks = [lastw[k] for k in reads if k in lastw]
+        for k in writes:
+            if k in lastw and not (accum and lastw[k][3] == qn):
+                toks.append(lastw[k])
+            toks += readers.get(k, [])
+        sync_to(qn, toks)
+
+    def record(tok, reads, writes):
+        for k in reads:
+            readers.setdefault(k, []).append(tok)
+        for k in writes:
+            lastw[k] = tok
+            readers[k] = []
+
+    def emit(qn, fn, reads, writes, accum=False):
+        deps(qn, reads, writes, accum)
+        s = psem[qn]
+        fn().then_inc(T.sem[s], 1)
+        done[qn] += 1
+        record((s, done[qn], dict(known[qn]), qn), reads, writes)
+
+    def dma(qn, out, in_, reads, writes):
+        deps(qn, reads, writes, False)
+        s = "dm%d" % ndma[0]
+        ndma[0] += 1
+        queue[qn].dma_start(out, in_).then_inc(T.sem[s], 16)
+        record((s, 16, dict(known[qn]), None), reads, writes)
+
+    def send(dst_ap, src_ap, sem, reads):
+        deps("G", reads, [], False)
+        tr = []
+        for d in cores:
+            if d == core:
+                continue
+            rid, pid, se = topo.addr(d)
+            es = eng[core][d]
+            tr.append(RemoteDMATransfer(src=src_ap, dst=dst_ap, dst_ids=[DstId(rid=rid, pnc=pid)],
+                                        dma_engine_mask=sum(1 << x for x in es), remote_sem=T.sem[sem]))
+            nsent[0] += len(es)
+        g.remote_dma_fused(tr, local_sem=T.sem.sent)
+
+    arrive = sum(len(eng[c][core]) for c in cores if c != core)
+    for t in range(DAYS):
+        lastw[("win", t, 0, "rem")] = ("al%d" % t, arrive, {}, None)
+        lastw[("win", t, 1, "rem")] = ("ah%d" % t, arrive, {}, None)
+        lastw[("cnt", t, "rem")] = ("ac%d" % t, arrive, {}, None)
+        lastw[("sw", t, "rem")] = ("as%d" % t, arrive, {}, None)
+
+    def ts(out, in0, s1, op0, r, w, s2=None, op1=None):
+        if op1 is None:
+            emit("V", lambda: g.vector.tensor_scalar(out, in0, s1, None, op0), r, w)
+        else:
+            emit("V", lambda: g.vector.tensor_scalar(out, in0, s1, s2, op0, op1), r, w)
+
+    def tt(out, a, b, op, r, w):
+        emit("V", lambda: g.vector.tensor_tensor(out, a, b, op), r, w)
+
+    def cpy(out, a, r, w):
+        emit("V", lambda: g.vector.tensor_copy(out, a), r, w)
+
+    def mmul(out, l, rhs, start, stop, r, w):
+        emit("P", lambda: g.tensor.matmul(out, l, rhs, start, stop), r, w, accum=not start)
+
+    def act(out, a, f, r, w, **kw):
+        emit("S", lambda: g.scalar.activation(out, a, f, **kw), r, w)
+
+    xs = [T.xa, T.xc]
+    ills = [T.ill0, T.ill1]
+    hs = [slice(0, H), slice(H, P)]
+    cs = [slice(0, 32), slice(32, 64)]
+    ks = [slice(0, 128), slice(128, 256)]
+    qs = [slice(n * 256, n * 256 + 256) for n in range(4)]
+
+    def nat(h, k):
+        return slice(64 * k + 32 * h, 64 * k + 32 * h + 32)
+
+    def own(h, k):
+        return slice(128 * h + 32 * k, 128 * h + 32 * k + 32)
+
+    for n in range(4):
+        dma("YS"[n % 2], T.xi[:, qs[n]], T.x0[:, qs[n]], [], [("xi", n)])
+    dma("Y", T.ni[:], T.nb[:], [], ["ni"])
+    dma("S", T.di[:], T.dice[:], [], ["di"])
+    dma("Y", T.ri[:], T.res[:], [], ["ri"])
+
+    emit("G", lambda: g.iota(T.t2[:], [[-16, 8], [0, 16]], 0, 1), [], ["t2"])
+    emit("G", lambda: g.iota(T.t1[:], [[-1, 128]], 0, 1), [], ["t1"])
+    emit("G", lambda: g.iota(T.vvc[:], [[16, 64]], 0, 0, allow_small_or_imprecise_dtypes=True), [], ["vvc"])
+    emit("G", lambda: g.iota(T.lo[:], [[0, 16], [1, 64]], 0, 0, allow_small_or_imprecise_dtypes=True), [], ["lo"])
+    emit("G", lambda: g.iota(T.dat[:], [[1, 16], [0, 64]], 16 * q, 0, allow_small_or_imprecise_dtypes=True), [], ["dat"])
+    emit("V", lambda: g.vector.memset(T.bp[:], 0.0), [], ["bp"])
+    emit("V", lambda: g.vector.memset(T.z64[:], 0.0), [], ["z64"])
+    ts(T.t2s[:], T.t2[:], 4, A.arith_shift_right, ["t2"], ["t2s"])
+    ts(T.t3[:], T.t1[:, 0:16], 15, A.bitwise_and, ["t1"], ["t3"])
+    ts(T.mb[:], T.t2s[:], 0, A.is_equal, ["t2s"], ["mb"])
+    ts(T.r16[:], T.t3[:], 0, A.is_equal, ["t3"], ["r16"], 256.0, A.mult)
+    cpy(T.bp[:, 16:144:16], T.mb[:, 0:128:16], ["mb"], ["bp"])
+    for i in range(16):
+        act(T.ex[:, i * 128:(i + 1) * 128], T.mb[:], F.Copy, ["mb", "r16"], [("ex", i)], scale=T.r16[:, i:i + 1])
+    ts(T.idn[:], T.t1[:], 0, A.is_equal, ["t1"], ["idn"])
+    ts(T.su1[:], T.t1[:], 0, A.is_gt, ["t1"], ["su1"], -1.0, A.mult)
+    ts(T.i2[:], T.t1[:], 0, A.is_equal, ["t1"], ["i2"], -2048.0, A.mult)
+    tt(T.su[:], T.su1[:], T.mb[:], A.mult, ["su1", "mb"], ["su"])
+    tt(T.su2[:], T.su[:], T.i2[:], A.add, ["su", "i2"], ["su2"])
+    for n in range(4):
+        cpy(T.xa[:, qs[n]], T.xi[:, qs[n]], [("xi", n)], [("x", 0, n // 2)])
+    dma("Y", T.dat[1:128:16, :], T.lo[0:8, :], ["lo"], ["dat"])
+    dma("Y", T.er[0:8, :], T.mb[0:128:16, :], ["mb"], ["er"])
+
+    def total(t, h):
+        x = xs[t % 2]
+        for i in range(16):
+            mmul(T["tc%d" % h][:, 0:32], T.bp[:, 16 - i:144 - i], x[:, h * H + i:(h + 1) * H:16], i == 0, i == 15,
+                 ["bp", ("x", t % 2, h)], [("tc", h)])
+
+    def high(t, h):
+        ts(T.high[:, cs[h]], T["tc%d" % h][:, 0:32], float(TH), A.is_ge, [("tc", h)], [("high", h)])
+
+    def running(t, h):
+        tc = T["tc%d" % h]
+        for n, l in ((1, "mb"), (2, "su2")):
+            mmul(tc[:, 32 * n:32 * n + 32], T[l][:], T.high[:, cs[h]], True, True, [l, ("high", h)], [("tc", h)])
+        if h == 1:
+            mmul(tc[:, 96:160], T.su[:], T.high[:], True, True, ["su", ("high", 0), ("high", 1)], [("tc", 1)])
+        mmul(T["e%d" % h][:], T.idn[:], xs[t % 2][:, hs[h]], True, False, ["idn", ("x", t % 2, h)], ["e%d" % h])
+
+    def infected(t, h):
+        tc, tk = T["tc%d" % h], ("tc", h)
+        init = 0.0 if h == 0 else T.pre[:, 31:32]
+        emit("V", lambda: g.vector.tensor_tensor_scan(T.pre[:, cs[h]], tc[:, 32:64], T.z64[:, 0:32], init, A.add, A.add),
+             [tk, "z64"] + [("pre", 0)] * h, [("pre", h)])
+        tt(T.zz[:, cs[h]], T.pre[:, cs[h]], tc[:, 64:96], A.add, [("pre", h), tk], [("zz", h)])
+        ts(ills[t % 2][:, cs[h]], T.zz[:, cs[h]], CAP - 2048 + 0.5, A.is_le, [("zz", h)], [("ill", t % 2, h)])
+
+    def spread(t, h):
+        e = T["e%d" % h]
+        for i in range(16):
+            mmul(e[:, i:H:16], T.ex[:, i * 128:(i + 1) * 128], ills[t % 2][:, cs[h]], False, i == 15,
+                 [("ex", i), ("ill", t % 2, h)], ["e%d" % h])
+
+    def mask(t, h):
+        o = T["win%d" % t][:, q * P + h * H:q * P + (h + 1) * H]
+        e = T["e%d" % h]
+        if MQ[h] == "V":
+            ts(o, e[:], -256.0, A.add, ["e%d" % h], [("win", t, h)], 0.0, A.max)
+        else:
+            act(o, e[:], F.Relu, ["e%d" % h], [("win", t, h)], bias=-256.0)
+        send(o, o, "%s%d" % (("al", "ah")[h], t), [("win", t, h)])
+
+    def counts(t, j):
+        b = 16 * t + 4 * q
+        c = T.cnt[:, b + 1:b + 2]
+        if j == 0:
+            ts(c, T.pre[:, 63:64], float(CAP), A.min, [("pre", 1)], [("cn", t, 1)])
+            return
+        ts(T.cnt[:, b:b + 1], c, -1.0 / 2048, A.mult, [("cn", t, 1)], [("cn", t, 0)], 0.5, A.add)
+        m, a = (1.0, EPS - 0.5) if q == 0 else (-1.0, 2047.5)
+        ts(T.cnt[:, b + 2:b + 3], c, m, A.mult, [("cn", t, 1)], [("cn", t, 2)], a, A.add)
+        s = T.cnt[:, b:b + 3]
+        send(s, s, "ac%d" % t, [("cn", t, 0), ("cn", t, 1), ("cn", t, 2)])
+
+    def spots(t, j):
+        ill = ills[t % 2]
+        ik = [("ill", t % 2, 0), ("ill", t % 2, 1)]
+        if j == 0:
+            tt(T.cum[:], T.pre[:], T.tc1[:, 96:160], A.add, [("pre", 0), ("pre", 1), ("tc", 1)], ["cum"])
+        elif j == 1:
+            if right:
+                ts(T.sel[:], ill[:], -float(P), A.mult, ik, ["sel"], float(P), A.add)
+            else:
+                ts(T.sel[:], ill[:], float(P), A.mult, ik, ["sel"])
+        elif j == 2:
+            if right:
+                ts(T.cum[:], T.cum[:], float(CAP), A.min, ["cum"], ["cum"], -float(CAP), A.add)
+            else:
+                ts(T.cum[:], T.cum[:], float(CAP), A.min, ["cum"], ["cum"])
+        elif j == 3:
+            tt(T.ee[:], T.sel[:], T.vv[:], A.min if right else A.max, ["sel", "vv"], ["ee"])
+        elif j == 4:
+            tt(T.pos[:], T.ee[:], T.cum[:], A.subtract, ["ee", "cum"], ["pos"])
+        elif right:
+            b = 16 * t + 4 * q
+            ts(T.pos16[:], T.pos[:], T.cnt[:, b + 1:b + 2], A.add, ["pos", ("cn", t, 1)], ["pos16"], -float(CAP), A.add)
+        else:
+            cpy(T.pos16[:], T.pos[:], ["pos"], ["pos16"])
+
+    def scatter(t):
+        seg = T["sw%d" % t][:, q * P:(q + 1) * P]
+        emit("V", lambda: g.vector.tensor_copy(seg.indirect(T.pos16[:, 0:64]), T.dat[:]), ["pos16", "dat"], [("sw", t, "own")])
+        send(seg, seg, "as%d" % t, [("sw", t, "own")])
+
+    def places(t, j):
+        b = 16 * t
+        rd = [("cn", t, 0), ("cn", t, 1), ("cn", t, 2), ("cnt", t, "rem")]
+        y = T.sl[:, 256:512]
+        if j == 0:
+            emit("V", lambda: g.vector.tensor_reduce(T.ka[:, t:t + 1], T.cnt[:, b:b + 13:4], X.X, A.add), rd, [("ka", t)])
+            emit("V", lambda: g.vector.tensor_reduce(T.kb[:, t:t + 1], T.cnt[:, b + 5:b + 10:4], X.X, A.add), rd, [("kb", t)])
+        elif j == 1:
+            ts(y, T["dd%d" % t][:], T.ka[:, t:t + 1], A.mult, [("dd", t), ("ka", t)] + rd, ["sl"], T.cnt[:, b + 2:b + 3], A.add)
+        elif j == 2:
+            ts(T.hh[:], y, T.cnt[:, b + 6:b + 7], A.is_ge, ["sl", ("kb", t)] + rd, ["hh"], T.kb[:, t:t + 1], A.mult)
+        elif j == 3:
+            tt(T.oi[:], y, T.hh[:], A.add, ["sl", "hh"], ["oi"])
+        else:
+            cpy(T["offs%d" % (t % 2)][:], T.oi[:], ["oi"], [("offs", t % 2)])
+
+    def sums(o, key, lhs, src, srck, h, i0, i1):
+        for i in range(i0, i1):
+            mmul(o, lhs[0][:, 16 - i:144 - i], src[:, h * 4 * H + i:(h + 1) * 4 * H:16], i == 0, False,
+                 [lhs[1]] + [(srck, k, h) for k in range(4)], [key])
+
+    def hits(t, h, part=None):
+        i0, i1 = (0, 16) if part is None else (8 * part, 8 * part + 8)
+        sums(T.ht[:, ks[h]], "ht", (T.bp, "bp"), T.raw, "raw", h, i0, i1)
+        if i1 == 16:
+            for k in range(4):
+                mmul(T.ht[:, own(h, k)], T.ineg[:], ills[t % 2][:, cs[h]], False, k == 3, ["ineg", ("ill", t % 2, h)], ["ht"])
+
+    SB = [("sl", T.sl), ("c1", T.c1)]
+
+    def slsum(t, h):
+        l = ("idn", "id2", "id3", "id4")[t]
+        b, B = SB[h]
+        o = B[:, ks[0]]
+        sums(o, b, (T.cp, "cp"), T.rsl, "rsl", h, 0, 16)
+        mmul(o, T[l][:], T.sg[:, ks[h]], False, True, [l, ("sg", h)], [b])
+
+    def fetch(qn, win, wk, offs, ok, out, outk, k, h):
+        o = out[:, h * 4 * H + k * H:h * 4 * H + (k + 1) * H]
+        s = win[:].indirect(offs[:, own(h, k)])
+        if qn == "V":
+            cpy(o, s, wk + [ok], [(outk, k, h)])
+        else:
+            act(o, s, F.Copy, wk + [ok], [(outk, k, h)])
+
+    def gather(t, k, h):
+        wk = [("win", t, 0), ("win", t, 1), ("win", t, 0, "rem"), ("win", t, 1, "rem")]
+        fetch((LQ if t < DAYS - 1 else LQL)["%d%d" % (k, h)], T["win%d" % t], wk, T.off, ("off", h), T.raw, "raw", k, h)
+
+    def slfetch(t, k, h):
+        wk = [("sw", t, "own"), ("sw", t, "rem")]
+        fetch((SQ if t < DAYS - 1 else SQL)["%d%d" % (k, h)], T["sw%d" % t], wk, T["offs%d" % (t % 2)], ("offs", t % 2),
+              T.rsl, "rsl", k, h)
+
+    banks = ["c0", "c1"]
+    nb = [0]
+
+    def bank():
+        nb[0] += 1
+        return banks[(nb[0] - 1) % 2]
+
+    def raws(k, h):
+        return T.raw[:, h * 4 * H + k * H:h * 4 * H + (k + 1) * H]
+
+    def lift(k, h):
+        b = bank()
+        mmul(T[b][:], T.idn[:], raws(k, h), True, True, ["idn", ("raw", k, h)], [b])
+        a = raws(0, h) if k == 1 else T.mm[:, hs[h]]
+        tt(T.mm[:, hs[h]], a, T[b][:], A.max, [("raw", 0, h) if k == 1 else ("mm", h), b], [("mm", h)])
+
+    def resist(h):
+        mmul(T["e%d" % h][:], T.er[:], T.rneg[:, hs[h]], True, False, ["er", "rneg"], ["e%d" % h])
+
+    def less(h):
+        mmul(T["e%d" % h][:], T.idn[:], T.mm[:, hs[h]], False, True, ["idn", ("mm", h)], ["e%d" % h])
+        tt(T.xm[:, hs[h]], T.xm[:, hs[h]], T["e%d" % h][:], A.max, [("xm", h), "e%d" % h], [("xm", h)])
+
+    def newx(t, h):
+        last = t == DAYS - 1
+        nx = (t + 1) % 2
+        o = T.yo if last else xs[nx]
+        b = bank()
+        mmul(T[b][:], T.er[:], T.rneg[:, hs[h]], True, False, ["er", "rneg"], [b])
+        mmul(T[b][:], T.idn[:], raws(3, h), False, True, ["idn", ("raw", 3, h)], [b])
+        tt(o[:, hs[h]], T.xm[:, hs[h]], T[b][:], A.max, [("xm", h), b], [("yo", h) if last else ("x", nx, h)])
+        if last:
+            dma("Y", T.yx[:, hs[h]], T.yo[:, hs[h]], [("yo", h)], [("yx", h)])
+
+    def fade(t, h):
+        ts(T.xm[:, hs[h]], xs[t % 2][:, hs[h]], -8.0, A.add, [("x", t % 2, h)], [("xm", h)], 0.0, A.max)
+
+    def struck(h):
+        act(T.sg[:, ks[h]], T.ht[:, ks[h]], F.Sign, ["ht"], [("sg", h)], bias=-float(TH) / 2)
+
+    def ll(h):
+        return T.tc1[:, 256 + 128 * h:384 + 128 * h]
+
+    def keep(h):
+        tt(T.lk[:, ks[h]], ll(h), T.sg[:, ks[h]], A.subtract, [("tc", 1), ("sg", h)], [("lk", h)])
+
+    def renew(t, h):
+        b, B = SB[h]
+        if t < DAYS - 1:
+            tt(ll(h), T.lk[:, ks[h]], B[:, ks[0]], A.max, [("lk", h), b], [("tc", 1)])
+            return
+        tt(T.lk[:, ks[h]], T.lk[:, ks[h]], B[:, ks[0]], A.max, [("lk", h), b], [("lk", h)])
+        for k in range(4):
+            if k % 2:
+                act(T.no[:, nat(h, k)], T.lk[:, own(h, k)], F.Copy, [("lk", h)], [("no", h, k)], scale=SH, bias=-(t + 1) * SH)
+            else:
+                ts(T.no[:, nat(h, k)], T.lk[:, own(h, k)], -(t + 1.0), A.add, [("lk", h)], [("no", h, k)], SH, A.mult)
+
+    def offnew(t, h):
+        ts(T.off[:, ks[h]], ll(h), -(t + 1.0), A.add, [("tc", 1)], [("off", h)], SH, A.mult)
+
+    def number():
+        ts(T.pmi[:], T.t1[:, 0:1], 15, A.bitwise_and, ["t1"], ["pmi"])
+        cpy(T.pmf[:, 0:1], T.pmi[:], ["pmi"], ["pmf"])
+        ts(T.vv[:], T.vvc[:], T.pmf[:, 0:1], A.add, ["vvc", "pmf"], ["vv"])
+
+    def offsets():
+        for h in (0, 1):
+            for k in range(4):
+                cpy(T.off[:, own(h, k)], T.ni[:, nat(h, k)], ["ni"], [("off", h, k)])
+            lastw[("off", h)] = lastw[("off", h, 3)]
+
+    def draws():
+        for h in (0, 1):
+            for k in range(4):
+                cpy(T.dd0[:, own(h, k)], T.di[:, nat(h, k)], ["di"], [("dd0", h, k)])
+        lastw[("dd", 0)] = lastw[("dd0", 1, 3)]
+        for t in range(1, DAYS):
+            ts(T.dtmp[:], T.dd0[:], STEP * t, A.add, [("dd", 0)], ["dtmp"])
+            ts(T["dd%d" % t][:], T.dtmp[:], M2, A.bitwise_and, ["dtmp"], [("dd", t)])
+
+    def misc():
+        ts(T.rw[:], T.ri[:], -1.0, A.mult, ["ri"], ["rw"])
+        dma("Y", T.rneg[0:8, :], T.rw[:], ["rw"], ["rneg"])
+        act(T.pmf[:, 1:2], T.r16[:, 1:2], F.Copy, ["r16"], ["pmf1"], scale=1.0 / 256 / SH)
+        act(T.ineg[:], T.idn[:], F.Copy, ["idn"], ["ineg"], scale=-SH)
+        act(T.pmf[:, 2:3], T.r16[:, 0:1], F.Identity, ["r16", "pmf1"], ["pmf2"], scale=64.0 / 256 / SH, bias=T.pmf[:, 1:2])
+        for n in (2, 3, 4):
+            act(T["id%d" % n][:], T.idn[:], F.Copy, ["idn"], ["id%d" % n], scale=float(n))
+        act(T.cp[:], T.bp[:], F.Copy, ["bp", "pmf2"], ["cp"], scale=T.pmf[:, 2:3])
+        ts(T.nf[:], T.ni[:], 1.0 / SH, A.mult, ["ni"], ["nf"])
+        for h in (0, 1):
+            for k in range(4):
+                act(T.tc1[:, 256 + 128 * h + 32 * k:288 + 128 * h + 32 * k], T.nf[:, nat(h, k)], F.Copy, ["nf"], [("tc", 1)])
+        draws()
+
+    once = {"num": number, "off": offsets, "misc": misc}
+    flags = {"T": total, "a": high, "F": running, "v": infected, "s": spread, "m": mask, "C": counts, "Z": spots, "M": scatter,
+             "D": fade}
+    halves = {"l": lift, "r": resist, "b": less, "u": struck, "K": keep}
+    both = {"g": gather, "k": slfetch, "n": newx, "S": slsum, "R": renew, "O": offnew, "h": hits, "p": places}
+
+    def run(t, order):
+        for n in order.split():
+            a = [int(c) for c in n[1:] if c.isdigit()]
+            if n in once:
+                once[n]()
+            elif n[0] in flags:
+                flags[n[0]](t + 1, *a)
+            elif n[0] in halves:
+                halves[n[0]](*a)
+            else:
+                both[n[0]](t, *a)
+
+    run(-1, FIRST)
+    for t in range(DAYS - 1):
+        run(t, DAY)
+    run(DAYS - 1, LAST)
+    dma("Y", T.ynb[:], T.no[:], [("no", h, k) for h in (0, 1) for k in range(4)], ["ynb"])
+
+    sync_to("G", [lastw["ynb"], lastw[("yx", 0)], lastw[("yx", 1)]])
+    for k in ("V", "S", "P", "G"):
+        g.wait_ge(T.sem[psem[k]], done[k])
+    g.wait_ge(T.sem.sent, nsent[0])

@@ -1,20 +1,19 @@
 from concourse.bass import DstId, RemoteDMATransfer
-from concourse.mybir import AluOpType as A, ActivationFunctionType as F, AxisListType as X
+from concourse.mybir import AluOpType as A, ActivationFunctionType as F
 
 DAYS, P, CAP, TH, STEP, M2 = 4, 1024, 384, 1200, 77, 2047
-H = 512
+CUT = (0, 32, 64)
 EPS = 2.0 ** -12
 SH = 8192.0
-LQ = {"00": "V", "10": "S", "20": "S", "30": "S", "01": "S", "11": "S", "21": "S", "31": "S"}
-SQ = {"00": "S", "10": "S", "20": "S", "30": "S", "01": "S", "11": "S", "21": "S", "31": "S"}
-LQL = {"00": "S", "10": "V", "20": "V", "30": "S", "01": "S", "11": "S", "21": "S", "31": "S"}
-SQL = {"00": "S", "10": "S", "20": "S", "30": "V", "01": "S", "11": "V", "21": "V", "31": "S"}
-MQ = "VS"
-FIRST = """T0 a0 F0 T1 num D1 v0 a1 off s0 m0 F1 v1 misc Z0 Z1 s1 Z2 m1 Z3 C0 Z4 D0 Z5 C1 M"""
-DAY = """g00 g10 g20 l10 l20 p0 r0 p1 g11 r1 b0 g30 g01 n0 l11 p2 h00 T0 a0 g21 l21 p3 F0 h01 v0 g31 p4 b1 n1 s0 u0 T1 k31 m0
- k20 a1 D1 F1 k11 D0 v1 k10 s1 k00 Z0 m1 Z1 Z2 k30 C0 k21 Z3 h1 k01 C1 S0 u1 Z4 K0 Z5 M R0 O0 S1 K1 R1 O1"""
-LAST = """g10 g30 g00 g20 p0 g11 r0 g01 l10 p1 l20 h00 p2 l11 p3 b0 p4 g31 n0 h01 g21 l21 u0 k10 k30 r1 k00 k11 k20 k01 k31 b1
- h1 u1 k21 n1 K1 S0 K0 S1 R0 R1"""
+TOP = 2048.0
+LIFT = (EPS - 0.5, -2047.5, 2047.5, -4096 + 0.5 - EPS)
+C0 = 4080 / SH
+BG = 2944
+FIRST = """T0 a0 F0 T1 num v0 a1 i0 one s0 F1 m0V v1 i1 s1 blk m1V C Z0 Z1 off res M0 M1 slots D0V D1V misc d1 d2 d3 w1 w2 w3"""
+DAY = """g00V g01S g02V g03S c0 g10S h0 g11S T0 h1 p0 g13V g12S a0 F0 p1 v0 p2 i0 s0 c1 m0S h2 T1 p3 p4 a1 F1 v1 i1 s1 k00S
+ k11S m1V C Z0 h3 D0V Z1 k55V M0 u03 k44V M1 K03 k23S S01 D1V k66S k77S R01 O01 S22 S33 R22 O22 R33 O33"""
+LAST = """g00V g01S g02V g03S c0 g10S h0 g11S h1 p0 g13V g12S p1 p2 h2 h3 p3 p4 y0S c1 k01S u03 k45V y1S K03 k23S S01 k66V
+ k77S R01 O01 S22 S33 R22 O22 R33 O33"""
 
 
 def _sb(dtype, *names, cols, rows=128):
@@ -23,33 +22,39 @@ def _sb(dtype, *names, cols, rows=128):
 
 SCRATCH = {}
 SCRATCH.update(_sb("int32", "xi", cols=P))
-SCRATCH.update(_sb("int32", "ni", "di", "dtmp", "oi", "dd0", "dd1", "dd2", "dd3", cols=256))
+SCRATCH.update(_sb("int32", "ni", "dd0", "dtmp", "oi", "dd1", "dd2", "dd3", cols=256))
 SCRATCH.update(_sb("int32", "t1", "t2", "t2s", cols=128))
 SCRATCH.update(_sb("int32", "ri", cols=64))
 SCRATCH.update(_sb("int32", "t3", cols=16))
 SCRATCH.update(_sb("int32", "pmi", cols=1))
 SCRATCH.update(_sb("uint16", "off", "offs0", "offs1", cols=256))
-SCRATCH.update(_sb("uint16", "pos16", cols=64))
-SCRATCH.update(_sb("bfloat16", "xa", "xc", "xm", "mm", "dat", cols=P))
-SCRATCH.update(_sb("bfloat16", "raw", "rsl", cols=4 * P))
+SCRATCH.update(_sb("uint16", "bo", cols=4))
+SCRATCH.update(_sb("bfloat16", "slot", "xs", "step", cols=5 * P))
+SCRATCH.update(_sb("bfloat16", "rsl", cols=4 * P))
 SCRATCH.update(_sb("bfloat16", *["win%d" % _t for _t in range(DAYS)], *["sw%d" % _t for _t in range(DAYS)], cols=4 * P))
-SCRATCH.update(_sb("bfloat16", "rneg", "lo", cols=P, rows=8))
+SCRATCH.update(_sb("bfloat16", "bg", cols=BG))
+SCRATCH.update(_sb("bfloat16", "up", cols=P))
+SCRATCH.update(_sb("bfloat16", "rneg", cols=P, rows=8))
 SCRATCH.update(_sb("bfloat16", "er", cols=128, rows=8))
 SCRATCH.update(_sb("bfloat16", "ex", cols=2048))
 SCRATCH.update(_sb("bfloat16", "sg", cols=256))
-SCRATCH.update(_sb("bfloat16", "bp", "cp", cols=144))
-SCRATCH.update(_sb("bfloat16", "mb", "idn", "id2", "id3", "id4", "ineg", "su", "su1", "i2", "su2", cols=128))
-SCRATCH.update(_sb("bfloat16", "high", "ill0", "ill1", "rw", cols=64))
+SCRATCH.update(_sb("bfloat16", "bp", "cp", "bn", cols=144))
+SCRATCH.update(_sb("bfloat16", "mb", "idn", "id2", "id3", "id4", "ineg", "su", "su1", "i2", "lt", cols=128))
+SCRATCH.update(_sb("bfloat16", "high", "ill0", "ill1", "rw", "cc", "cq", "cd", "dm", "rl", "top", cols=64))
+SCRATCH.update(_sb("bfloat16", "c16", cols=4))
+SCRATCH.update(_sb("float16", "pre", cols=66))
 SCRATCH.update(_sb("float32", "yo", cols=P))
-SCRATCH.update(_sb("float32", "no", "lk", "hh", "nf", cols=256))
-SCRATCH.update(_sb("float32", "pre", "zz", "cum", "ee", "pos", "z64", "vvc", "vv", "sel", cols=64))
+SCRATCH.update(_sb("float32", "no", "lk", "hh", cols=256))
 SCRATCH.update(_sb("float32", "cnt", cols=16 * DAYS))
 SCRATCH.update(_sb("float32", "r16", cols=16))
-SCRATCH.update(_sb("float32", "pmf", "ka", "kb", cols=4))
-for _b in ("c0", "c1", "e0", "e1", "ht", "sl", "tc0", "tc1"):
+SCRATCH.update(_sb("float32", "col", cols=8))
+SCRATCH.update(_sb("float32", "m16", "ka", "kb", "junk", cols=4))
+BANKS = ("ta", "tb", "cn", "e0", "e1", "ht", "sl0", "sl1")
+for _b in BANKS:
     SCRATCH[_b] = ("psum", [128, 512], "float32")
-SEMAPHORES = ["pv", "ps", "pp", "pg", "sent"] + ["dm%d" % i for i in range(16)]
-SEMAPHORES += [k + "%d" % t for k in ("al", "ah", "ac", "as") for t in range(DAYS)]
+SEMAPHORES = ["pv", "ps", "pp", "pg", "sent"] + ["dm%d" % i for i in range(20)]
+SEMAPHORES += ["al%d_%d" % (t, p) for t in range(DAYS) for p in range(len(CUT) - 1)]
+SEMAPHORES += [k + "%d" % t for k in ("ac", "as") for t in range(DAYS)]
 
 
 def plan(topo, cores, src):
@@ -81,8 +86,10 @@ def rank_program(g, core, T, topo):
     done = {k: 0 for k in queue}
     known = {k: {} for k in queue}
     lastw, readers = {}, {}
+    visit = {b: {} for b in BANKS}
     ndma = [0]
     nsent = [0]
+    NP = len(CUT) - 1
 
     def sync_to(qn, toks):
         need = {}
@@ -103,12 +110,17 @@ def rank_program(g, core, T, topo):
             if known[qn].get(s, 0) < v:
                 known[qn][s] = v
 
+    def banks(keys):
+        return {k[0] for k in keys if isinstance(k, tuple) and k[0] in visit}
+
     def deps(qn, reads, writes, accum):
         toks = [lastw[k] for k in reads if k in lastw]
         for k in writes:
             if k in lastw and not (accum and lastw[k][3] == qn):
                 toks.append(lastw[k])
             toks += readers.get(k, [])
+        for b in banks(reads + writes):
+            toks += [t for o, t in visit[b].items() if o != qn]
         sync_to(qn, toks)
 
     def record(tok, reads, writes):
@@ -117,6 +129,8 @@ def rank_program(g, core, T, topo):
         for k in writes:
             lastw[k] = tok
             readers[k] = []
+        for b in banks(reads + writes):
+            visit[b][tok[3]] = tok
 
     def emit(qn, fn, reads, writes, accum=False):
         deps(qn, reads, writes, accum)
@@ -132,7 +146,7 @@ def rank_program(g, core, T, topo):
         queue[qn].dma_start(out, in_).then_inc(T.sem[s], 16)
         record((s, 16, dict(known[qn]), None), reads, writes)
 
-    def send(dst_ap, src_ap, sem, reads):
+    def send(ap, sem, reads):
         deps("G", reads, [], False)
         tr = []
         for d in cores:
@@ -140,15 +154,15 @@ def rank_program(g, core, T, topo):
                 continue
             rid, pid, se = topo.addr(d)
             es = eng[core][d]
-            tr.append(RemoteDMATransfer(src=src_ap, dst=dst_ap, dst_ids=[DstId(rid=rid, pnc=pid)],
+            tr.append(RemoteDMATransfer(src=ap, dst=ap, dst_ids=[DstId(rid=rid, pnc=pid)],
                                         dma_engine_mask=sum(1 << x for x in es), remote_sem=T.sem[sem]))
             nsent[0] += len(es)
         g.remote_dma_fused(tr, local_sem=T.sem.sent)
 
     arrive = sum(len(eng[c][core]) for c in cores if c != core)
     for t in range(DAYS):
-        lastw[("win", t, 0, "rem")] = ("al%d" % t, arrive, {}, None)
-        lastw[("win", t, 1, "rem")] = ("ah%d" % t, arrive, {}, None)
+        for p in range(NP):
+            lastw[("win", t, p, "rem")] = ("al%d_%d" % (t, p), arrive, {}, None)
         lastw[("cnt", t, "rem")] = ("ac%d" % t, arrive, {}, None)
         lastw[("sw", t, "rem")] = ("as%d" % t, arrive, {}, None)
 
@@ -164,38 +178,65 @@ def rank_program(g, core, T, topo):
     def cpy(out, a, r, w):
         emit("V", lambda: g.vector.tensor_copy(out, a), r, w)
 
+    def fill(out, c, w):
+        emit("V", lambda: g.vector.memset(out, c), [], w)
+
+    def scan(out, d0, d1, init, op0, op1, r, w):
+        emit("V", lambda: g.vector.tensor_tensor_scan(out, d0, d1, init, op0, op1), r, w)
+
     def mmul(out, l, rhs, start, stop, r, w):
         emit("P", lambda: g.tensor.matmul(out, l, rhs, start, stop), r, w, accum=not start)
 
     def act(out, a, f, r, w, **kw):
         emit("S", lambda: g.scalar.activation(out, a, f, **kw), r, w)
 
-    xs = [T.xa, T.xc]
+    def iota(out, pattern, base, mult, w, **kw):
+        emit("G", lambda: g.iota(out, pattern, base, mult, **kw), [], w)
+
+    def relu(qn, out, a, r, w, bias=0.0):
+        if qn == "S":
+            act(out, a, F.Relu, r, w, bias=bias)
+        elif bias:
+            ts(out, a, bias, A.add, r, w, 0.0, A.max)
+        else:
+            ts(out, a, 0.0, A.max, r, w)
+
     ills = [T.ill0, T.ill1]
-    hs = [slice(0, H), slice(H, P)]
-    cs = [slice(0, 32), slice(32, 64)]
-    ks = [slice(0, 128), slice(128, 256)]
-    qs = [slice(n * 256, n * 256 + 256) for n in range(4)]
+    cs = [slice(CUT[p], CUT[p + 1]) for p in range(NP)]
+    hs = [slice(16 * CUT[p], 16 * CUT[p + 1]) for p in range(NP)]
+    parts, nth = [], 0
+    for p in range(NP):
+        parts.append([])
+        for a in range(CUT[p], CUT[p + 1], 32):
+            parts[p].append((a, min(a + 32, CUT[p + 1]), "e%d" % (nth % 2)))
+            nth += 1
 
-    def nat(h, k):
-        return slice(64 * k + 32 * h, 64 * k + 32 * h + 32)
+    def slots(buf, a, b, k, every=1):
+        return buf[:, 5 * a + k:5 * b:5 * every]
 
-    def own(h, k):
-        return slice(128 * h + 32 * k, 128 * h + 32 * k + 32)
+    XK = [("x", p) for p in range(NP)]
 
-    for n in range(4):
-        dma("YS"[n % 2], T.xi[:, qs[n]], T.x0[:, qs[n]], [], [("xi", n)])
-    dma("Y", T.ni[:], T.nb[:], [], ["ni"])
-    dma("S", T.di[:], T.dice[:], [], ["di"])
+    def illk(t):
+        return [("ill", t % 2, p) for p in range(NP)]
+
+    load = []
+    for p in range(NP):
+        a, b = 16 * CUT[p], 16 * CUT[p + 1]
+        load += [(p, a, (a + b) // 2), (p, (a + b) // 2, b)]
+    for n, (p, a, b) in enumerate(load):
+        dma("YS"[n % 2], T.xi[:, a:b], T.x0[:, a:b], [], [("xi", n)])
     dma("Y", T.ri[:], T.res[:], [], ["ri"])
+    dma("S", T.ni[:], T.nb[:], [], ["ni"])
+    dma("Y", T.dd0[:], T.dice[:], [], [("dd", 0)])
 
-    emit("G", lambda: g.iota(T.t2[:], [[-16, 8], [0, 16]], 0, 1), [], ["t2"])
-    emit("G", lambda: g.iota(T.t1[:], [[-1, 128]], 0, 1), [], ["t1"])
-    emit("G", lambda: g.iota(T.vvc[:], [[16, 64]], 0, 0, allow_small_or_imprecise_dtypes=True), [], ["vvc"])
-    emit("G", lambda: g.iota(T.lo[:], [[0, 16], [1, 64]], 0, 0, allow_small_or_imprecise_dtypes=True), [], ["lo"])
-    emit("G", lambda: g.iota(T.dat[:], [[1, 16], [0, 64]], 16 * q, 0, allow_small_or_imprecise_dtypes=True), [], ["dat"])
-    emit("V", lambda: g.vector.memset(T.bp[:], 0.0), [], ["bp"])
-    emit("V", lambda: g.vector.memset(T.z64[:], 0.0), [], ["z64"])
+    small = dict(allow_small_or_imprecise_dtypes=True)
+    iota(T.t2[:], [[-16, 8], [0, 16]], 0, 1, ["t2"])
+    iota(T.t1[:], [[-1, 128]], 0, 1, ["t1"])
+    iota(T.cc[:], [[1, 64]], 0, 0, ["cc"], **small)
+    iota(T.m16[:], [[16, 4]], 0, 0, ["m16"], **small)
+    iota(T.bg[:, 0:P], [[0, P]], 1, 0, ["bg"], **small)
+    fill(T.bp[:], 0.0, ["bp"])
+    fill(T.top[:], TOP, ["top"])
     ts(T.t2s[:], T.t2[:], 4, A.arith_shift_right, ["t2"], ["t2s"])
     ts(T.t3[:], T.t1[:, 0:16], 15, A.bitwise_and, ["t1"], ["t3"])
     ts(T.mb[:], T.t2s[:], 0, A.is_equal, ["t2s"], ["mb"])
@@ -204,272 +245,253 @@ def rank_program(g, core, T, topo):
     for i in range(16):
         act(T.ex[:, i * 128:(i + 1) * 128], T.mb[:], F.Copy, ["mb", "r16"], [("ex", i)], scale=T.r16[:, i:i + 1])
     ts(T.idn[:], T.t1[:], 0, A.is_equal, ["t1"], ["idn"])
-    ts(T.su1[:], T.t1[:], 0, A.is_gt, ["t1"], ["su1"], -1.0, A.mult)
-    ts(T.i2[:], T.t1[:], 0, A.is_equal, ["t1"], ["i2"], -2048.0, A.mult)
+    ts(T.su1[:], T.t1[:], 0, A.is_lt, ["t1"], ["su1"], -1.0, A.mult)
+    ts(T.i2[:], T.t1[:], 0, A.is_equal, ["t1"], ["i2"], TOP, A.mult)
+    ts(T.pre[:, 0:1], T.top[:, 0:1], -float(CAP), A.add, ["top"], ["pre0"])
     tt(T.su[:], T.su1[:], T.mb[:], A.mult, ["su1", "mb"], ["su"])
-    tt(T.su2[:], T.su[:], T.i2[:], A.add, ["su", "i2"], ["su2"])
-    for n in range(4):
-        cpy(T.xa[:, qs[n]], T.xi[:, qs[n]], [("xi", n)], [("x", 0, n // 2)])
-    dma("Y", T.dat[1:128:16, :], T.lo[0:8, :], ["lo"], ["dat"])
+    for n, (p, a, b) in enumerate(load):
+        cpy(slots(T.xs, a, b, 4), T.xi[:, a:b], [("xi", n)], [("x", p)])
     dma("Y", T.er[0:8, :], T.mb[0:128:16, :], ["mb"], ["er"])
 
-    def total(t, h):
-        x = xs[t % 2]
+    def tbank(p):
+        return ("ta", "tb")[p % 2]
+
+    def total(t, p):
+        a, b = CUT[p], CUT[p + 1]
         for i in range(16):
-            mmul(T["tc%d" % h][:, 0:32], T.bp[:, 16 - i:144 - i], x[:, h * H + i:(h + 1) * H:16], i == 0, i == 15,
-                 ["bp", ("x", t % 2, h)], [("tc", h)])
+            mmul(T[tbank(p)][:, 0:b - a], T.bp[:, 16 - i:144 - i], slots(T.xs, 16 * a + i, 16 * b, 4, 16), i == 0, i == 15,
+                 ["bp", ("x", p)], [(tbank(p),)])
 
-    def high(t, h):
-        ts(T.high[:, cs[h]], T["tc%d" % h][:, 0:32], float(TH), A.is_ge, [("tc", h)], [("high", h)])
+    def high(t, p):
+        ts(T.high[:, cs[p]], T[tbank(p)][:, 0:CUT[p + 1] - CUT[p]], float(TH), A.is_ge, [(tbank(p),)], [("high", p)])
 
-    def running(t, h):
-        tc = T["tc%d" % h]
-        for n, l in ((1, "mb"), (2, "su2")):
-            mmul(tc[:, 32 * n:32 * n + 32], T[l][:], T.high[:, cs[h]], True, True, [l, ("high", h)], [("tc", h)])
-        if h == 1:
-            mmul(tc[:, 96:160], T.su[:], T.high[:], True, True, ["su", ("high", 0), ("high", 1)], [("tc", 1)])
-        mmul(T["e%d" % h][:], T.idn[:], xs[t % 2][:, hs[h]], True, False, ["idn", ("x", t % 2, h)], ["e%d" % h])
+    def running(t, p):
+        a, b = CUT[p], CUT[p + 1]
+        mmul(T.cn[:, a:b], T.mb[:], T.high[:, a:b], True, True, ["mb", ("high", p)], [("cn", "sum", p)])
+        mmul(T.cn[:, 64 + a:64 + b], T.su[:], T.high[:, a:b], True, False, ["su", ("high", p)], [("cn", "in", p)])
+        mmul(T.cn[:, 64 + a:64 + b], T.i2[:], T.high[:, a:b], False, True, ["i2", ("high", p)], [("cn", "in", p)])
+        a, b, e = parts[p][0]
+        mmul(T[e][:, 0:16 * (b - a)], T.idn[:], slots(T.xs, 16 * a, 16 * b, 4), True, False, ["idn", ("x", p)], [(e,)])
 
-    def infected(t, h):
-        tc, tk = T["tc%d" % h], ("tc", h)
-        init = 0.0 if h == 0 else T.pre[:, 31:32]
-        emit("V", lambda: g.vector.tensor_tensor_scan(T.pre[:, cs[h]], tc[:, 32:64], T.z64[:, 0:32], init, A.add, A.add),
-             [tk, "z64"] + [("pre", 0)] * h, [("pre", h)])
-        tt(T.zz[:, cs[h]], T.pre[:, cs[h]], tc[:, 64:96], A.add, [("pre", h), tk], [("zz", h)])
-        ts(ills[t % 2][:, cs[h]], T.zz[:, cs[h]], CAP - 2048 + 0.5, A.is_le, [("zz", h)], [("ill", t % 2, h)])
+    def counted(t, p):
+        b = CUT[p + 1]
+        scan(T.pre[:, 1:b + 1], T.cn[:, 0:b], T.top[:, 0:b], TOP - CAP, A.add, A.min,
+             ["top"] + [("cn", "sum", o) for o in range(p + 1)], ["pre"])
 
-    def spread(t, h):
-        e = T["e%d" % h]
+    def infected(t, p):
+        a, b = CUT[p], CUT[p + 1]
+        tt(ills[t % 2][:, a:b], T.pre[:, a:b], T.cn[:, 64 + a:64 + b], A.is_lt, ["pre", "pre0", ("cn", "in", p)],
+           [("ill", t % 2, p)])
+
+    def spread(t, p, n=0):
+        a, b, e = parts[p][n]
+        if n:
+            mmul(T[e][:, 0:16 * (b - a)], T.idn[:], slots(T.xs, 16 * a, 16 * b, 4), True, False, ["idn", ("x", p)], [(e,)])
         for i in range(16):
-            mmul(e[:, i:H:16], T.ex[:, i * 128:(i + 1) * 128], ills[t % 2][:, cs[h]], False, i == 15,
-                 [("ex", i), ("ill", t % 2, h)], ["e%d" % h])
+            mmul(T[e][:, i:16 * (b - a):16], T.ex[:, i * 128:(i + 1) * 128], ills[t % 2][:, a:b], False, i == 15,
+                 [("ex", i), ("ill", t % 2, p)], [(e,)])
 
-    def mask(t, h):
-        o = T["win%d" % t][:, q * P + h * H:q * P + (h + 1) * H]
-        e = T["e%d" % h]
-        if MQ[h] == "V":
-            ts(o, e[:], -256.0, A.add, ["e%d" % h], [("win", t, h)], 0.0, A.max)
-        else:
-            act(o, e[:], F.Relu, ["e%d" % h], [("win", t, h)], bias=-256.0)
-        send(o, o, "%s%d" % (("al", "ah")[h], t), [("win", t, h)])
+    def mask(t, p, *how):
+        n = how[0] if len(how) > 1 else 0
+        a, b, e = parts[p][n]
+        W = T["win%d" % t]
+        relu(how[-1], W[:, q * P + 16 * a:q * P + 16 * b], T[e][:, 0:16 * (b - a)], [(e,)], [("win", t, p, n)], -256.0)
+        if n == len(parts[p]) - 1:
+            send(W[:, q * P + 16 * CUT[p]:q * P + 16 * CUT[p + 1]], "al%d_%d" % (t, p), [("win", t, p, o) for o in range(n + 1)])
 
-    def counts(t, j):
-        b = 16 * t + 4 * q
-        c = T.cnt[:, b + 1:b + 2]
-        if j == 0:
-            ts(c, T.pre[:, 63:64], float(CAP), A.min, [("pre", 1)], [("cn", t, 1)])
-            return
-        ts(T.cnt[:, b:b + 1], c, -1.0 / 2048, A.mult, [("cn", t, 1)], [("cn", t, 0)], 0.5, A.add)
-        m, a = (1.0, EPS - 0.5) if q == 0 else (-1.0, 2047.5)
-        ts(T.cnt[:, b + 2:b + 3], c, m, A.mult, [("cn", t, 1)], [("cn", t, 2)], a, A.add)
-        s = T.cnt[:, b:b + 3]
-        send(s, s, "ac%d" % t, [("cn", t, 0), ("cn", t, 1), ("cn", t, 2)])
+    def counts(t):
+        c = T.cnt[:, 16 * t + 4 * q:16 * t + 4 * q + 1]
+        ts(c, T.pre[:, 64:65], CAP - TOP, A.add, ["pre"], [("cnt", t)], LIFT[q], A.add)
+        send(c, "ac%d" % t, [("cnt", t)])
 
-    def spots(t, j):
+    def blocks(t, j):
         ill = ills[t % 2]
-        ik = [("ill", t % 2, 0), ("ill", t % 2, 1)]
         if j == 0:
-            tt(T.cum[:], T.pre[:], T.tc1[:, 96:160], A.add, [("pre", 0), ("pre", 1), ("tc", 1)], ["cum"])
-        elif j == 1:
-            if right:
-                ts(T.sel[:], ill[:], -float(P), A.mult, ik, ["sel"], float(P), A.add)
-            else:
-                ts(T.sel[:], ill[:], float(P), A.mult, ik, ["sel"])
-        elif j == 2:
-            if right:
-                ts(T.cum[:], T.cum[:], float(CAP), A.min, ["cum"], ["cum"], -float(CAP), A.add)
-            else:
-                ts(T.cum[:], T.cum[:], float(CAP), A.min, ["cum"], ["cum"])
-        elif j == 3:
-            tt(T.ee[:], T.sel[:], T.vv[:], A.min if right else A.max, ["sel", "vv"], ["ee"])
-        elif j == 4:
-            tt(T.pos[:], T.ee[:], T.cum[:], A.subtract, ["ee", "cum"], ["pos"])
-        elif right:
+            for o, l, c in ((192, "mb", "cq"), (128, "lt", "cd")):
+                mmul(T.cn[:, o:o + 64], T[l][:], ill[:], True, False, [l] + illk(t), [("cn", o)])
+                mmul(T.cn[:, o:o + 64], T.idn[:], T[c][:], False, True, ["idn", c], [("cn", o)])
+            act(T.rl[:], T.cn[:, 192:256], F.Relu, [("cn", 192)], ["rl"], scale=128.0, bias=-1984.0)
+            act(T.dm[:], T.cn[:, 128:192], F.Copy, [("cn", 128)], ["dm"])
+            return
+        o = T.ta[:, 64:68]
+        mmul(o, T.idn[:], T.c16[:], True, False, ["idn", "c16"], [("ta", "r")])
+        for i in range(16):
+            mmul(o, T.bn[:, 16 - i:144 - i], T.pre[:, i:64:16], False, False, ["bn", "pre", "pre0"], [("ta", "r")])
+        for i in range(16):
+            mmul(o, T.bp[:, 16 - i:144 - i], T.rl[:, i:64:16], False, i == 15, ["bp", "rl"], [("ta", "r")])
+        if right:
             b = 16 * t + 4 * q
-            ts(T.pos16[:], T.pos[:], T.cnt[:, b + 1:b + 2], A.add, ["pos", ("cn", t, 1)], ["pos16"], -float(CAP), A.add)
+            ts(T.bo[:], o, T.cnt[:, b:b + 1], A.add, [("ta", "r"), ("cnt", t)], ["bo"], TOP - CAP - LIFT[q], A.add)
         else:
-            cpy(T.pos16[:], T.pos[:], ["pos"], ["pos16"])
+            ts(T.bo[:], o, TOP - CAP, A.add, [("ta", "r")], ["bo"])
 
-    def scatter(t):
+    def spell(t, j):
+        if j == 0:
+            cpy(T.bg[:].indirect(T.bo[:]), T.dm[:], ["bo", "dm"], ["bg"])
+            return
         seg = T["sw%d" % t][:, q * P:(q + 1) * P]
-        emit("V", lambda: g.vector.tensor_copy(seg.indirect(T.pos16[:, 0:64]), T.dat[:]), ["pos16", "dat"], [("sw", t, "own")])
-        send(seg, seg, "as%d" % t, [("sw", t, "own")])
+        scan(seg, T.up[:], T.bg[:, 0:P], 1.0, A.add, A.min, ["up", "bg"], [("sw", t, "own")])
+        send(seg, "as%d" % t, [("sw", t, "own")])
+        if t < DAYS - 1:
+            iota(T.bg[:, 0:P], [[0, P]], 1, 0, ["bg"], **small)
+
+    def fade(t, p, qn):
+        relu(qn, slots(T.slot, 16 * CUT[p], 16 * CUT[p + 1], 4), slots(T.xs, 16 * CUT[p], 16 * CUT[p + 1], 4), [("x", p)],
+             [("slot", p, 4)], -8.0)
 
     def places(t, j):
         b = 16 * t
-        rd = [("cn", t, 0), ("cn", t, 1), ("cn", t, 2), ("cnt", t, "rem")]
-        y = T.sl[:, 256:512]
+        rd = [("cnt", t), ("cnt", t, "rem")]
+        y = T.sl0[:, 256:512]
         if j == 0:
-            emit("V", lambda: g.vector.tensor_reduce(T.ka[:, t:t + 1], T.cnt[:, b:b + 13:4], X.X, A.add), rd, [("ka", t)])
-            emit("V", lambda: g.vector.tensor_reduce(T.kb[:, t:t + 1], T.cnt[:, b + 5:b + 10:4], X.X, A.add), rd, [("kb", t)])
+            act(T.junk[:], T.cnt[:, b:b + 13:4], F.Copy, rd, [("ka", t), "junk"], scale=1.0 / 2048, accum_out=T.ka[:, t:t + 1])
+            act(T.kb[:, t:t + 1], T.cnt[:, b + 4:b + 5], F.Identity, rd, [("kb", t)], bias=T.cnt[:, b + 8:b + 9])
         elif j == 1:
-            ts(y, T["dd%d" % t][:], T.ka[:, t:t + 1], A.mult, [("dd", t), ("ka", t)] + rd, ["sl"], T.cnt[:, b + 2:b + 3], A.add)
+            ts(y, T["dd%d" % t][:], T.ka[:, t:t + 1], A.mult, [("dd", t), ("ka", t)] + rd, [("sl0", "y")], T.cnt[:, b:b + 1],
+               A.subtract)
         elif j == 2:
-            ts(T.hh[:], y, T.cnt[:, b + 6:b + 7], A.is_ge, ["sl", ("kb", t)] + rd, ["hh"], T.kb[:, t:t + 1], A.mult)
+            ts(T.hh[:], y, T.cnt[:, b + 4:b + 5], A.is_le, [("sl0", "y"), ("kb", t)] + rd, ["hh"], T.kb[:, t:t + 1], A.mult)
         elif j == 3:
-            tt(T.oi[:], y, T.hh[:], A.add, ["sl", "hh"], ["oi"])
+            tt(T.oi[:], T.hh[:], y, A.subtract, [("sl0", "y"), "hh"], ["oi"])
         else:
             cpy(T["offs%d" % (t % 2)][:], T.oi[:], ["oi"], [("offs", t % 2)])
 
-    def sums(o, key, lhs, src, srck, h, i0, i1):
-        for i in range(i0, i1):
-            mmul(o, lhs[0][:, 16 - i:144 - i], src[:, h * 4 * H + i:(h + 1) * 4 * H:16], i == 0, False,
-                 [lhs[1]] + [(srck, k, h) for k in range(4)], [key])
+    def gather(t, p, k, qn):
+        wk = [("win", t, o, n) for o in range(NP) for n in range(len(parts[o]))] + [("win", t, o, "rem") for o in range(NP)]
+        s = T["win%d" % t][:].indirect(T.off[:, 64 * k + CUT[p]:64 * k + CUT[p + 1]])
+        relu(qn, slots(T.slot, 16 * CUT[p], 16 * CUT[p + 1], k), s, wk + [("off", k)], [("slot", p, k)])
 
-    def hits(t, h, part=None):
-        i0, i1 = (0, 16) if part is None else (8 * part, 8 * part + 8)
-        sums(T.ht[:, ks[h]], "ht", (T.bp, "bp"), T.raw, "raw", h, i0, i1)
-        if i1 == 16:
-            for k in range(4):
-                mmul(T.ht[:, own(h, k)], T.ineg[:], ills[t % 2][:, cs[h]], False, k == 3, ["ineg", ("ill", t % 2, h)], ["ht"])
+    def newx(t, p):
+        a, b = 80 * CUT[p], 80 * CUT[p + 1]
+        scan(T.xs[:, a:b], T.step[:, a:b], T.slot[:, a:b], 0.0, A.add, A.max,
+             ["step0", "step1", "step4"] + [("slot", p, k) for k in range(5)], [("x", p)])
 
-    SB = [("sl", T.sl), ("c1", T.c1)]
+    def result(t, p, qn):
+        relu(qn, T.yo[:, hs[p]], slots(T.xs, 16 * CUT[p], 16 * CUT[p + 1], 4), [("x", p)], [("yo", p)])
+        dma("Y", T.yx[:, hs[p]], T.yo[:, hs[p]], [("yo", p)], [("yx", p)])
 
-    def slsum(t, h):
+    def slfetch(t, a, b, qn):
+        s = T["sw%d" % t][:].indirect(T["offs%d" % (t % 2)][:, 32 * a:32 * b + 32])
+        relu(qn, T.rsl[:, 512 * a:512 * b + 512], s, [("sw", t, "own"), ("sw", t, "rem"), ("offs", t % 2)],
+             [("rsl", u) for u in range(a, b + 1)])
+
+    def hits(t, k):
+        o = T.ht[:, 64 * k:64 * k + 64]
+        mmul(o, T.ineg[:], ills[t % 2][:], True, False, ["ineg"] + illk(t), [("ht", k)])
+        for i in range(16):
+            mmul(o, T.bp[:, 16 - i:144 - i], slots(T.slot, i, P, k, 16), False, i == 15,
+                 ["bp"] + [("slot", p, k) for p in range(NP)], [("ht", k)])
+
+    def ks(a, b, base=0):
+        return slice(base + 64 * a, base + 64 * b + 64)
+
+    def keys(a, b, *name):
+        return [name + (k,) for k in range(a, b + 1)]
+
+    SB = ("sl0", "e0", "sl1", "e1")
+
+    def slsum(t, a, b):
         l = ("idn", "id2", "id3", "id4")[t]
-        b, B = SB[h]
-        o = B[:, ks[0]]
-        sums(o, b, (T.cp, "cp"), T.rsl, "rsl", h, 0, 16)
-        mmul(o, T[l][:], T.sg[:, ks[h]], False, True, [l, ("sg", h)], [b])
+        o = T[SB[a]][:, ks(0, b - a)]
+        mmul(o, T[l][:], T.sg[:, ks(a, b)], True, False, [l] + keys(a, b, "sg"), [(SB[a], "s")])
+        for i in range(16):
+            mmul(o, T.cp[:, 16 - i:144 - i], T.rsl[:, 1024 * a + i:1024 * (b + 1):16], False, i == 15,
+                 ["cp"] + [("rsl", u) for u in range(2 * a, 2 * b + 2)], [(SB[a], "s")])
 
-    def fetch(qn, win, wk, offs, ok, out, outk, k, h):
-        o = out[:, h * 4 * H + k * H:h * 4 * H + (k + 1) * H]
-        s = win[:].indirect(offs[:, own(h, k)])
-        if qn == "V":
-            cpy(o, s, wk + [ok], [(outk, k, h)])
-        else:
-            act(o, s, F.Copy, wk + [ok], [(outk, k, h)])
+    def struck(t, a, b):
+        act(T.sg[:, ks(a, b)], T.ht[:, ks(a, b)], F.Sign, keys(a, b, "ht"), keys(a, b, "sg"), bias=-float(TH) / 2)
 
-    def gather(t, k, h):
-        wk = [("win", t, 0), ("win", t, 1), ("win", t, 0, "rem"), ("win", t, 1, "rem")]
-        fetch((LQ if t < DAYS - 1 else LQL)["%d%d" % (k, h)], T["win%d" % t], wk, T.off, ("off", h), T.raw, "raw", k, h)
+    def keep(t, a, b):
+        tt(T.lk[:, ks(a, b)], T.ht[:, ks(a, b, 256)], T.sg[:, ks(a, b)], A.subtract, keys(a, b, "ht", "ll") + keys(a, b, "sg"),
+           keys(a, b, "lk"))
 
-    def slfetch(t, k, h):
-        wk = [("sw", t, "own"), ("sw", t, "rem")]
-        fetch((SQ if t < DAYS - 1 else SQL)["%d%d" % (k, h)], T["sw%d" % t], wk, T["offs%d" % (t % 2)], ("offs", t % 2),
-              T.rsl, "rsl", k, h)
-
-    banks = ["c0", "c1"]
-    nb = [0]
-
-    def bank():
-        nb[0] += 1
-        return banks[(nb[0] - 1) % 2]
-
-    def raws(k, h):
-        return T.raw[:, h * 4 * H + k * H:h * 4 * H + (k + 1) * H]
-
-    def lift(k, h):
-        b = bank()
-        mmul(T[b][:], T.idn[:], raws(k, h), True, True, ["idn", ("raw", k, h)], [b])
-        a = raws(0, h) if k == 1 else T.mm[:, hs[h]]
-        tt(T.mm[:, hs[h]], a, T[b][:], A.max, [("raw", 0, h) if k == 1 else ("mm", h), b], [("mm", h)])
-
-    def resist(h):
-        mmul(T["e%d" % h][:], T.er[:], T.rneg[:, hs[h]], True, False, ["er", "rneg"], ["e%d" % h])
-
-    def less(h):
-        mmul(T["e%d" % h][:], T.idn[:], T.mm[:, hs[h]], False, True, ["idn", ("mm", h)], ["e%d" % h])
-        tt(T.xm[:, hs[h]], T.xm[:, hs[h]], T["e%d" % h][:], A.max, [("xm", h), "e%d" % h], [("xm", h)])
-
-    def newx(t, h):
-        last = t == DAYS - 1
-        nx = (t + 1) % 2
-        o = T.yo if last else xs[nx]
-        b = bank()
-        mmul(T[b][:], T.er[:], T.rneg[:, hs[h]], True, False, ["er", "rneg"], [b])
-        mmul(T[b][:], T.idn[:], raws(3, h), False, True, ["idn", ("raw", 3, h)], [b])
-        tt(o[:, hs[h]], T.xm[:, hs[h]], T[b][:], A.max, [("xm", h), b], [("yo", h) if last else ("x", nx, h)])
-        if last:
-            dma("Y", T.yx[:, hs[h]], T.yo[:, hs[h]], [("yo", h)], [("yx", h)])
-
-    def fade(t, h):
-        ts(T.xm[:, hs[h]], xs[t % 2][:, hs[h]], -8.0, A.add, [("x", t % 2, h)], [("xm", h)], 0.0, A.max)
-
-    def struck(h):
-        act(T.sg[:, ks[h]], T.ht[:, ks[h]], F.Sign, ["ht"], [("sg", h)], bias=-float(TH) / 2)
-
-    def ll(h):
-        return T.tc1[:, 256 + 128 * h:384 + 128 * h]
-
-    def keep(h):
-        tt(T.lk[:, ks[h]], ll(h), T.sg[:, ks[h]], A.subtract, [("tc", 1), ("sg", h)], [("lk", h)])
-
-    def renew(t, h):
-        b, B = SB[h]
+    def renew(t, a, b):
+        new = T[SB[a]][:, ks(0, b - a)]
         if t < DAYS - 1:
-            tt(ll(h), T.lk[:, ks[h]], B[:, ks[0]], A.max, [("lk", h), b], [("tc", 1)])
-            return
-        tt(T.lk[:, ks[h]], T.lk[:, ks[h]], B[:, ks[0]], A.max, [("lk", h), b], [("lk", h)])
-        for k in range(4):
-            if k % 2:
-                act(T.no[:, nat(h, k)], T.lk[:, own(h, k)], F.Copy, [("lk", h)], [("no", h, k)], scale=SH, bias=-(t + 1) * SH)
-            else:
-                ts(T.no[:, nat(h, k)], T.lk[:, own(h, k)], -(t + 1.0), A.add, [("lk", h)], [("no", h, k)], SH, A.mult)
+            tt(T.ht[:, ks(a, b, 256)], T.lk[:, ks(a, b)], new, A.max, keys(a, b, "lk") + [(SB[a], "s")], keys(a, b, "ht", "ll"))
+        else:
+            tt(T.lk[:, ks(a, b)], T.lk[:, ks(a, b)], new, A.max, keys(a, b, "lk") + [(SB[a], "s")], keys(a, b, "lk"))
 
-    def offnew(t, h):
-        ts(T.off[:, ks[h]], ll(h), -(t + 1.0), A.add, [("tc", 1)], [("off", h)], SH, A.mult)
+    def offnew(t, a, b):
+        if t < DAYS - 1:
+            ts(T.off[:, ks(a, b)], T.ht[:, ks(a, b, 256)], C0 - t - 1, A.add, keys(a, b, "ht", "ll"), keys(a, b, "off"), SH, A.mult)
+        else:
+            ts(T.no[:, ks(a, b)], T.lk[:, ks(a, b)], C0 - t - 1, A.add, keys(a, b, "lk"), keys(a, b, "no"), SH, A.mult)
+            dma("Y", T.ynb[:, ks(a, b)], T.no[:, ks(a, b)], keys(a, b, "no"), keys(a, b, "ynb"))
+
+    last = T.r16[:, 15:16]
 
     def number():
-        ts(T.pmi[:], T.t1[:, 0:1], 15, A.bitwise_and, ["t1"], ["pmi"])
-        cpy(T.pmf[:, 0:1], T.pmi[:], ["pmi"], ["pmf"])
-        ts(T.vv[:], T.vvc[:], T.pmf[:, 0:1], A.add, ["vvc", "pmf"], ["vv"])
-
-    def offsets():
-        for h in (0, 1):
-            for k in range(4):
-                cpy(T.off[:, own(h, k)], T.ni[:, nat(h, k)], ["ni"], [("off", h, k)])
-            lastw[("off", h)] = lastw[("off", h, 3)]
-
-    def draws():
-        for h in (0, 1):
-            for k in range(4):
-                cpy(T.dd0[:, own(h, k)], T.di[:, nat(h, k)], ["di"], [("dd0", h, k)])
-        lastw[("dd", 0)] = lastw[("dd0", 1, 3)]
-        for t in range(1, DAYS):
-            ts(T.dtmp[:], T.dd0[:], STEP * t, A.add, [("dd", 0)], ["dtmp"])
-            ts(T["dd%d" % t][:], T.dtmp[:], M2, A.bitwise_and, ["dtmp"], [("dd", t)])
-
-    def misc():
         ts(T.rw[:], T.ri[:], -1.0, A.mult, ["ri"], ["rw"])
         dma("Y", T.rneg[0:8, :], T.rw[:], ["rw"], ["rneg"])
-        act(T.pmf[:, 1:2], T.r16[:, 1:2], F.Copy, ["r16"], ["pmf1"], scale=1.0 / 256 / SH)
+        ts(T.pmi[:], T.t1[:, 0:1], 15, A.bitwise_and, ["t1"], ["pmi"])
+        tt(T.lt[:], T.idn[:], T.su[:], A.subtract, ["idn", "su"], ["lt"])
+        cpy(T.col[:, 0:1], T.pmi[:], ["pmi"], ["col0"])
+        fill(T.lt[:, 15:128:16], 0.0, ["lt"])
+
+    def offsets():
+        cpy(T.off[:], T.ni[:], ["ni"], keys(0, 3, "off"))
+
+    def one():
+        ts(T.col[:, 1:2], last, (15 + (255.0 - 64 * q) / 256) / 256, A.mult, ["r16", "col0"], ["col1"], T.col[:, 0:1], A.subtract)
+        ts(T.c16[:], T.m16[:], T.col[:, 0:1], A.add, ["m16", "col0"], ["c16"], 16.0, A.mult)
+
+    def blk():
+        act(T.col[:, 2:3], last, F.Copy, ["r16"], ["col2"], scale=-1.0 / 65536)
+        act(T.cq[:], T.cc[:], F.Copy, ["cc"], ["cq"], scale=1.0 / 256)
+        act(T.col[:, 3:4], last, F.Copy, ["r16"], ["col3"], scale=-1.0 / 256, bias=1.0)
+        act(T.cd[:], T.cc[:], F.Identity, ["cc", "col1", "col2"], ["cd"], scale=T.col[:, 2:3], bias=T.col[:, 1:2])
+        act(T.bn[:], T.bp[:], F.Copy, ["bp"], ["bn"], scale=-1.0 / 16)
+        act(T.up[:], T.bg[:, 0:P], F.Copy, ["bg", "col3"], ["up"], scale=T.col[:, 3:4])
+
+    def resist():
+        for n in (0, 1):
+            e = "e%d" % n
+            mmul(T[e][:], T.er[:], T.rneg[:, 512 * n:512 * n + 512], True, True, ["er", "rneg"], [(e,)])
+            act(slots(T.step, 512 * n, 512 * n + 512, 4), T[e][:], F.Copy, [(e,)], ["step4"])
+
+    def steps():
+        fill(slots(T.step, 0, P, 0), -1024.0, ["step0"])
+        fill(slots(T.step, 0, P, 1), 0.0, ["step1"])
+        for k in (2, 3):
+            act(slots(T.step, 0, P, k), T.up[:], F.Copy, ["up"], ["step4"], scale=0.0)
+
+    def misc():
+        act(T.col[:, 4:5], last, F.Copy, ["r16"], ["col4"], scale=-(0.5 + 1 / SH) / 256, bias=1 / SH)
         act(T.ineg[:], T.idn[:], F.Copy, ["idn"], ["ineg"], scale=-SH)
-        act(T.pmf[:, 2:3], T.r16[:, 0:1], F.Identity, ["r16", "pmf1"], ["pmf2"], scale=64.0 / 256 / SH, bias=T.pmf[:, 1:2])
+        act(T.cp[:], T.bp[:], F.Copy, ["bp", "col4"], ["cp"], scale=T.col[:, 4:5])
         for n in (2, 3, 4):
             act(T["id%d" % n][:], T.idn[:], F.Copy, ["idn"], ["id%d" % n], scale=float(n))
-        act(T.cp[:], T.bp[:], F.Copy, ["bp", "pmf2"], ["cp"], scale=T.pmf[:, 2:3])
-        ts(T.nf[:], T.ni[:], 1.0 / SH, A.mult, ["ni"], ["nf"])
-        for h in (0, 1):
-            for k in range(4):
-                act(T.tc1[:, 256 + 128 * h + 32 * k:288 + 128 * h + 32 * k], T.nf[:, nat(h, k)], F.Copy, ["nf"], [("tc", 1)])
-        draws()
+        ts(T.ht[:, 256:512], T.ni[:], 1.0 / SH, A.mult, ["ni"], keys(0, 3, "ht", "ll"), -C0, A.add)
 
-    once = {"num": number, "off": offsets, "misc": misc}
-    flags = {"T": total, "a": high, "F": running, "v": infected, "s": spread, "m": mask, "C": counts, "Z": spots, "M": scatter,
-             "D": fade}
-    halves = {"l": lift, "r": resist, "b": less, "u": struck, "K": keep}
-    both = {"g": gather, "k": slfetch, "n": newx, "S": slsum, "R": renew, "O": offnew, "h": hits, "p": places}
+    def draws(t, n):
+        ts(T["dd%d" % n][:], T.dd0[:], STEP * n, A.add, [("dd", 0)], [("dd", n)])
+
+    def wrap(t, n):
+        ts(T["dd%d" % n][:], T["dd%d" % n][:], M2, A.bitwise_and, [("dd", n)], [("dd", n)])
+
+    once = {"num": number, "off": offsets, "one": one, "blk": blk, "res": resist, "slots": steps, "misc": misc}
+    flags = {"T": total, "a": high, "F": running, "v": counted, "i": infected, "s": spread, "m": mask, "C": counts,
+             "Z": blocks, "M": spell, "D": fade}
+    day = {"g": gather, "c": newx, "y": result, "k": slfetch, "S": slsum, "u": struck, "K": keep, "R": renew, "O": offnew,
+           "h": hits, "p": places, "d": draws, "w": wrap}
 
     def run(t, order):
         for n in order.split():
-            a = [int(c) for c in n[1:] if c.isdigit()]
+            a = [int(c) if c.isdigit() else c for c in n[1:]]
             if n in once:
                 once[n]()
             elif n[0] in flags:
                 flags[n[0]](t + 1, *a)
-            elif n[0] in halves:
-                halves[n[0]](*a)
             else:
-                both[n[0]](t, *a)
+                day[n[0]](t, *a)
 
     run(-1, FIRST)
     for t in range(DAYS - 1):
         run(t, DAY)
     run(DAYS - 1, LAST)
-    dma("Y", T.ynb[:], T.no[:], [("no", h, k) for h in (0, 1) for k in range(4)], ["ynb"])
 
-    sync_to("G", [lastw["ynb"], lastw[("yx", 0)], lastw[("yx", 1)]])
+    sync_to("G", [lastw[k] for k in keys(0, 3, "ynb")] + [lastw[("yx", p)] for p in range(NP)])
     for k in ("V", "S", "P", "G"):
         g.wait_ge(T.sem[psem[k]], done[k])
     g.wait_ge(T.sem.sent, nsent[0])

@@ -2,18 +2,20 @@ from concourse.bass import DstId, RemoteDMATransfer
 from concourse.mybir import AluOpType as A, ActivationFunctionType as F
 
 DAYS, P, CAP, TH, STEP, M2 = 4, 1024, 384, 1200, 77, 2047
-CUT = (0, 32, 64)
-EPS = 2.0 ** -12
-SH = 8192.0
+RUN = 128
 TOP = 2048.0
-LIFT = (EPS - 0.5, -2047.5, 2047.5, -4096 + 0.5 - EPS)
-C0 = 4080 / SH
-BG = 2944
-FIRST = """T0 a0 F0 T1 num v0 a1 i0 one s0 F1 m0V v1 i1 s1 blk m1V C Z0 Z1 off res M0 M1 slots D0V D1V misc d1 d2 d3 w1 w2 w3"""
-DAY = """g00V g01S g02V g03S c0 g10S h0 g11S T0 h1 p0 g13V g12S a0 F0 p1 v0 p2 i0 s0 c1 m0S h2 T1 p3 p4 a1 F1 v1 i1 s1 k00S
- k11S m1V C Z0 h3 D0V Z1 k55V M0 u03 k44V M1 K03 k23S S01 D1V k66S k77S R01 O01 S22 S33 R22 O22 R33 O33"""
-LAST = """g00V g01S g02V g03S c0 g10S h0 g11S h1 p0 g13V g12S p1 p2 h2 h3 p3 p4 y0S c1 k01S u03 k45V y1S K03 k23S S01 k66V
- k77S R01 O01 S22 S33 R22 O22 R33 O33"""
+BG = 3456
+WIDE = 48
+PAD = WIDE - 8
+LOAD = "02Y rS 25S 58Y nY dS"
+FIRST = """z1S z2S b11 b10 b08 b06 x02 q020 q021 T02 l02 a02 s02 E28 num m02S W02 x25 l25 x58 T28 b03 l58 a28 z3S F28 b09 i28 s25
+ s58 b12 b02 m25S m58V W28 D04V b14 rise b07 L0 D48S d3 O04 b01 b04 b05 blk res L1 d1 b13 b00 misc L2 C B w3 d2 w2 Z0 w1 z0V Z1
+ Z3 Z2V Z5 M0 M1 N"""
+DAY = """H23 g030V g031S g033V p0 p1 g032S H02 H34 c03 q030 g363S g360S g362V T03 g361S l03 q031 g683S g682S s03 m03S W03 h3 c36
+ a03 g680S p2 T36 g681S l36 E36 a36 p3 F36 i36 p4 h0 s36 h1 k01S c68 m36V W36 T68 k12S E68 a68 F68 i68 l68 s68 D04V m68V W68 h2
+ k34S L0 k23V L1 D48V k45S Z0 L2 C S01 Z2V Z1 k56V Z3 S12 Z5 M0 S23 M1 N R02 k78S R23 k67S S34 A02 O02 R34 A24 O24"""
+LAST = """g040V p0 p1 g481S g042V p2 H01 g480S H12 g041S g043S g482S p3 c04 p4 g483S c48 k01V h0 k12S H34 k56V h3 y04G h1 H23 h2
+ k45S S01 k23S S23 k67V R23 A23 R01 k34S S12 R12 A02 y48G O23 O02 k78S S34 R34 A34 O34"""
 
 
 def _sb(dtype, *names, cols, rows=128):
@@ -22,7 +24,7 @@ def _sb(dtype, *names, cols, rows=128):
 
 SCRATCH = {}
 SCRATCH.update(_sb("int32", "xi", cols=P))
-SCRATCH.update(_sb("int32", "ni", "dd0", "dtmp", "oi", "dd1", "dd2", "dd3", cols=256))
+SCRATCH.update(_sb("int32", "ni", "dd0", "oi", "dd1", "dd2", "dd3", cols=256))
 SCRATCH.update(_sb("int32", "t1", "t2", "t2s", cols=128))
 SCRATCH.update(_sb("int32", "ri", cols=64))
 SCRATCH.update(_sb("int32", "t3", cols=16))
@@ -36,24 +38,28 @@ SCRATCH.update(_sb("bfloat16", "bg", cols=BG))
 SCRATCH.update(_sb("bfloat16", "up", cols=P))
 SCRATCH.update(_sb("bfloat16", "rneg", cols=P, rows=8))
 SCRATCH.update(_sb("bfloat16", "er", cols=128, rows=8))
-SCRATCH.update(_sb("bfloat16", "ex", cols=2048))
-SCRATCH.update(_sb("bfloat16", "sg", cols=256))
-SCRATCH.update(_sb("bfloat16", "bp", "cp", "bn", cols=144))
-SCRATCH.update(_sb("bfloat16", "mb", "idn", "id2", "id3", "id4", "ineg", "su", "su1", "i2", "lt", cols=128))
-SCRATCH.update(_sb("bfloat16", "high", "ill0", "ill1", "rw", "cc", "cq", "cd", "dm", "rl", "top", cols=64))
-SCRATCH.update(_sb("bfloat16", "c16", cols=4))
-SCRATCH.update(_sb("float16", "pre", cols=66))
+SCRATCH.update(_sb("bfloat16", "ee", "big", cols=16 * WIDE, rows=WIDE))
+SCRATCH.update(_sb("bfloat16", "it", cols=P, rows=WIDE))
+SCRATCH.update(_sb("bfloat16", "hi", cols=PAD + 64))
+SCRATCH.update(_sb("bfloat16", "zb", cols=40))
+SCRATCH.update(_sb("bfloat16", "w2", cols=128, rows=64))
+SCRATCH.update(_sb("bfloat16", "bp", "cp", "bn", "hb", cols=144))
+SCRATCH.update(_sb("bfloat16", "mb", "mq", "idn", "idk", "ineg", "su1", "i2", "lt", "qq", "top", cols=128))
+SCRATCH.update(_sb("bfloat16", "ill0", "ill1", "rw", "cc", "cd", "dm", cols=64))
+SCRATCH.update(_sb("bfloat16", "m16", cols=67))
+SCRATCH.update(_sb("float16", "cq", "rl", cols=64))
+SCRATCH.update(_sb("float16", "cst", cols=8))
+SCRATCH.update(_sb("int32", "csi", cols=8))
+SCRATCH.update(_sb("float16", "pre", cols=320 * DAYS))
 SCRATCH.update(_sb("float32", "yo", cols=P))
-SCRATCH.update(_sb("float32", "no", "lk", "hh", cols=256))
-SCRATCH.update(_sb("float32", "cnt", cols=16 * DAYS))
+SCRATCH.update(_sb("float32", "no", "hh", cols=256))
 SCRATCH.update(_sb("float32", "r16", cols=16))
 SCRATCH.update(_sb("float32", "col", cols=8))
-SCRATCH.update(_sb("float32", "m16", "ka", "kb", "junk", cols=4))
 BANKS = ("ta", "tb", "cn", "e0", "e1", "ht", "sl0", "sl1")
 for _b in BANKS:
     SCRATCH[_b] = ("psum", [128, 512], "float32")
-SEMAPHORES = ["pv", "ps", "pp", "pg", "sent"] + ["dm%d" % i for i in range(20)]
-SEMAPHORES += ["al%d_%d" % (t, p) for t in range(DAYS) for p in range(len(CUT) - 1)]
+SEMAPHORES = ["pv", "ps", "pp", "pg", "sent"] + ["dm%d" % i for i in range(24)]
+SEMAPHORES += ["al%d_%d" % (t, a) for t in range(DAYS) for a in range(8)]
 SEMAPHORES += [k + "%d" % t for k in ("ac", "as") for t in range(DAYS)]
 
 
@@ -68,7 +74,7 @@ def plan(topo, cores, src):
         e[d] = es[n * w:(n + 1) * w]
         used += e[d]
     for n, d in enumerate(near):
-        es = [x for x in topo.engines(src, d) if x not in used]
+        es = [x for x in topo.engines(src, d) if x not in used][::2]
         w = len(es) // len(near)
         e[d] = es[n * w:(n + 1) * w]
     return e
@@ -89,7 +95,6 @@ def rank_program(g, core, T, topo):
     visit = {b: {} for b in BANKS}
     ndma = [0]
     nsent = [0]
-    NP = len(CUT) - 1
 
     def sync_to(qn, toks):
         need = {}
@@ -149,20 +154,22 @@ def rank_program(g, core, T, topo):
     def send(ap, sem, reads):
         deps("G", reads, [], False)
         tr = []
-        for d in cores:
-            if d == core:
-                continue
+        for d, es in eng[core].items():
             rid, pid, se = topo.addr(d)
-            es = eng[core][d]
             tr.append(RemoteDMATransfer(src=ap, dst=ap, dst_ids=[DstId(rid=rid, pnc=pid)],
                                         dma_engine_mask=sum(1 << x for x in es), remote_sem=T.sem[sem]))
             nsent[0] += len(es)
         g.remote_dma_fused(tr, local_sem=T.sem.sent)
 
+    def keys(a, b, *name):
+        return [name + (k,) for k in range(a, b)]
+
     arrive = sum(len(eng[c][core]) for c in cores if c != core)
     for t in range(DAYS):
-        for p in range(NP):
-            lastw[("win", t, p, "rem")] = ("al%d_%d" % (t, p), arrive, {}, None)
+        for n in (DAY if t else FIRST).split():
+            if n[0] == "W":
+                for k in keys(int(n[1]), int(n[2]), "far", t):
+                    lastw[k] = ("al%d_%s" % (t, n[1]), arrive, {}, None)
         lastw[("cnt", t, "rem")] = ("ac%d" % t, arrive, {}, None)
         lastw[("sw", t, "rem")] = ("as%d" % t, arrive, {}, None)
 
@@ -202,267 +209,305 @@ def rank_program(g, core, T, topo):
             ts(out, a, 0.0, A.max, r, w)
 
     ills = [T.ill0, T.ill1]
-    cs = [slice(CUT[p], CUT[p + 1]) for p in range(NP)]
-    hs = [slice(16 * CUT[p], 16 * CUT[p + 1]) for p in range(NP)]
-    parts, nth = [], 0
-    for p in range(NP):
-        parts.append([])
-        for a in range(CUT[p], CUT[p + 1], 32):
-            parts[p].append((a, min(a + 32, CUT[p + 1]), "e%d" % (nth % 2)))
-            nth += 1
 
-    def slots(buf, a, b, k, every=1):
-        return buf[:, 5 * a + k:5 * b:5 * every]
+    def span(a, b, w=RUN, base=0):
+        return slice(base + w * a, base + w * b)
 
-    XK = [("x", p) for p in range(NP)]
+    def slots(buf, a, b, k, first=0, every=1):
+        return buf[:, 5 * (RUN * a + first) + k:5 * RUN * b:5 * every]
 
-    def illk(t):
-        return [("ill", t % 2, p) for p in range(NP)]
-
-    load = []
-    for p in range(NP):
-        a, b = 16 * CUT[p], 16 * CUT[p + 1]
-        load += [(p, a, (a + b) // 2), (p, (a + b) // 2, b)]
-    for n, (p, a, b) in enumerate(load):
-        dma("YS"[n % 2], T.xi[:, a:b], T.x0[:, a:b], [], [("xi", n)])
-    dma("Y", T.ri[:], T.res[:], [], ["ri"])
-    dma("S", T.ni[:], T.nb[:], [], ["ni"])
-    dma("Y", T.dd0[:], T.dice[:], [], [("dd", 0)])
+    whole = {"r": (T.ri, T.res, ["ri"]), "n": (T.ni, T.nb, keys(0, 4, "ni")), "d": (T.dd0, T.dice, [("dd", 0)])}
+    for n in LOAD.split():
+        if n[0] in whole:
+            dma(n[1], whole[n[0]][0][:], whole[n[0]][1][:], [], whole[n[0]][2])
+        else:
+            a, b = int(n[0]), int(n[1])
+            dma(n[2], T.xi[:, span(a, b)], T.x0[:, span(a, b)], [], keys(a, b, "xi"))
 
     small = dict(allow_small_or_imprecise_dtypes=True)
     iota(T.t2[:], [[-16, 8], [0, 16]], 0, 1, ["t2"])
     iota(T.t1[:], [[-1, 128]], 0, 1, ["t1"])
-    iota(T.cc[:], [[1, 64]], 0, 0, ["cc"], **small)
-    iota(T.m16[:], [[16, 4]], 0, 0, ["m16"], **small)
-    iota(T.bg[:, 0:P], [[0, P]], 1, 0, ["bg"], **small)
+    fill(T.big[:], 256.0, ["big"])
+    mmul(T.ht[:], T.big[:, 0:128], T.big[:, 0:512], True, True, ["big"], [("ht",)])
+    fill(T.hi[:, 0:PAD], 0.0, ["pad"])
+    fill(T.top[:], 1.0, ["top"])
     fill(T.bp[:], 0.0, ["bp"])
-    fill(T.top[:], TOP, ["top"])
+    fill(T.zb[:], 0.0, ["zb"])
+    emit("G", lambda: g.affine_select(T.ee[:], T.big[:], [[-1, WIDE], [0, 16]], A.is_equal, 0.0, 0, 1), ["big"], ["ee"])
     ts(T.t2s[:], T.t2[:], 4, A.arith_shift_right, ["t2"], ["t2s"])
-    ts(T.t3[:], T.t1[:, 0:16], 15, A.bitwise_and, ["t1"], ["t3"])
-    ts(T.mb[:], T.t2s[:], 0, A.is_equal, ["t2s"], ["mb"])
-    ts(T.r16[:], T.t3[:], 0, A.is_equal, ["t3"], ["r16"], 256.0, A.mult)
-    cpy(T.bp[:, 16:144:16], T.mb[:, 0:128:16], ["mb"], ["bp"])
-    for i in range(16):
-        act(T.ex[:, i * 128:(i + 1) * 128], T.mb[:], F.Copy, ["mb", "r16"], [("ex", i)], scale=T.r16[:, i:i + 1])
-    ts(T.idn[:], T.t1[:], 0, A.is_equal, ["t1"], ["idn"])
     ts(T.su1[:], T.t1[:], 0, A.is_lt, ["t1"], ["su1"], -1.0, A.mult)
+    ts(T.mb[:], T.t2s[:], 0, A.is_equal, ["t2s"], ["mb"])
     ts(T.i2[:], T.t1[:], 0, A.is_equal, ["t1"], ["i2"], TOP, A.mult)
-    ts(T.pre[:, 0:1], T.top[:, 0:1], -float(CAP), A.add, ["top"], ["pre0"])
-    tt(T.su[:], T.su1[:], T.mb[:], A.mult, ["su1", "mb"], ["su"])
-    for n, (p, a, b) in enumerate(load):
-        cpy(slots(T.xs, a, b, 4), T.xi[:, a:b], [("xi", n)], [("x", p)])
+    ts(T.idn[:], T.t1[:], 0, A.is_equal, ["t1"], ["idn"])
+    ts(T.t3[:], T.t1[:, 0:16], 15, A.bitwise_and, ["t1"], ["t3"])
+    tt(T.qq[:], T.su1[:], T.i2[:], A.add, ["su1", "i2"], ["qq"])
+    ts(T.r16[:], T.t3[:], 0, A.is_equal, ["t3"], ["r16"], 256.0, A.mult)
+    cpy(T.zb[:, 16:24], T.mb[:, 0:128:16], ["mb"], ["zb"])
+    cpy(T.bp[:, 16:144:16], T.mb[:, 0:128:16], ["mb"], ["bp"])
     dma("Y", T.er[0:8, :], T.mb[0:128:16, :], ["mb"], ["er"])
 
-    def tbank(p):
-        return ("ta", "tb")[p % 2]
+    def tally(t, r, a, b):
+        o = 80 * (4 * t + r)
+        return T.pre[:, o + a:o + b]
 
-    def total(t, p):
-        a, b = CUT[p], CUT[p + 1]
-        for i in range(16):
-            mmul(T[tbank(p)][:, 0:b - a], T.bp[:, 16 - i:144 - i], slots(T.xs, 16 * a + i, 16 * b, 4, 16), i == 0, i == 15,
-                 ["bp", ("x", p)], [(tbank(p),)])
+    def widen(t, a, b):
+        cpy(slots(T.xs, a, b, 4), T.xi[:, span(a, b)], keys(a, b, "xi"), keys(a, b, "x"))
 
-    def high(t, p):
-        ts(T.high[:, cs[p]], T[tbank(p)][:, 0:CUT[p + 1] - CUT[p]], float(TH), A.is_ge, [(tbank(p),)], [("high", p)])
+    piece, ebank, turn = {}, {}, [0, 0]
 
-    def running(t, p):
-        a, b = CUT[p], CUT[p + 1]
-        mmul(T.cn[:, a:b], T.mb[:], T.high[:, a:b], True, True, ["mb", ("high", p)], [("cn", "sum", p)])
-        mmul(T.cn[:, 64 + a:64 + b], T.su[:], T.high[:, a:b], True, False, ["su", ("high", p)], [("cn", "in", p)])
-        mmul(T.cn[:, 64 + a:64 + b], T.i2[:], T.high[:, a:b], False, True, ["i2", ("high", p)], [("cn", "in", p)])
-        a, b, e = parts[p][0]
-        mmul(T[e][:, 0:16 * (b - a)], T.idn[:], slots(T.xs, 16 * a, 16 * b, 4), True, False, ["idn", ("x", p)], [(e,)])
+    def total(t, a, b):
+        turn[0] = turn[0] + 1 if a else 0
+        bank = ("ta", "tb")[turn[0] % 2]
+        for r in range(a, b):
+            piece[r] = (a, b, turn[0] % 2)
+            mmul(T[bank][:, span(r - a, r - a + 1, 8)], slots(T.xs, r, r + 1, 4), T.mb[:, 0:128:16], True, True,
+                 ["mb", ("x", r)], [(bank, r - a)])
 
-    def counted(t, p):
-        b = CUT[p + 1]
-        scan(T.pre[:, 1:b + 1], T.cn[:, 0:b], T.top[:, 0:b], TOP - CAP, A.add, A.min,
-             ["top"] + [("cn", "sum", o) for o in range(p + 1)], ["pre"])
+    def lift(t, a, b):
+        turn[1] = turn[1] + 1 if a else 0
+        e = ebank[a] = "e%d" % (turn[1] % 2)
+        mmul(T[e][:, span(0, b - a)], T.idn[:], slots(T.xs, a, b, 4), True, False, ["idn"] + keys(a, b, "x"), [(e,)])
 
-    def infected(t, p):
-        a, b = CUT[p], CUT[p + 1]
-        tt(ills[t % 2][:, a:b], T.pre[:, a:b], T.cn[:, 64 + a:64 + b], A.is_lt, ["pre", "pre0", ("cn", "in", p)],
-           [("ill", t % 2, p)])
+    def high(t, a, b):
+        bank = ("ta", "tb")[piece[a][2]]
+        ts(T.hi[:, span(a, b, 8, PAD)], T[bank][:, span(0, b - a, 8)], float(TH), A.is_ge, keys(0, b - a, bank), keys(a, b, "hi"))
 
-    def spread(t, p, n=0):
-        a, b, e = parts[p][n]
-        if n:
-            mmul(T[e][:, 0:16 * (b - a)], T.idn[:], slots(T.xs, 16 * a, 16 * b, 4), True, False, ["idn", ("x", p)], [(e,)])
-        for i in range(16):
-            mmul(T[e][:, i:16 * (b - a):16], T.ex[:, i * 128:(i + 1) * 128], ills[t % 2][:, a:b], False, i == 15,
-                 [("ex", i), ("ill", t % 2, p)], [(e,)])
+    def carry(a, b, par, steps, start, stop):
+        bank = ("tb", "ta")[par]
+        for d in steps:
+            mmul(T[bank][0:8 * (b - a), 64:65], T.hi[:, span(a - d, b - d, 8, PAD)], T.top[:, 0:1], start and d == steps[0],
+                 stop and d == steps[-1], ["top", "pad"] + keys(0, b if stop else a, "hi"), [(bank, "c")])
 
-    def mask(t, p, *how):
-        n = how[0] if len(how) > 1 else 0
-        a, b, e = parts[p][n]
-        W = T["win%d" % t]
-        relu(how[-1], W[:, q * P + 16 * a:q * P + 16 * b], T[e][:, 0:16 * (b - a)], [(e,)], [("win", t, p, n)], -256.0)
-        if n == len(parts[p]) - 1:
-            send(W[:, q * P + 16 * CUT[p]:q * P + 16 * CUT[p + 1]], "al%d_%d" % (t, p), [("win", t, p, o) for o in range(n + 1)])
+    def within(a, b):
+        par = piece[a][2]
+        return T.cn[0:8 * (b - a), span(par, par + 1, RUN, 256)], ("cn", "in", par)
 
-    def counts(t):
-        c = T.cnt[:, 16 * t + 4 * q:16 * t + 4 * q + 1]
-        ts(c, T.pre[:, 64:65], CAP - TOP, A.add, ["pre"], [("cnt", t)], LIFT[q], A.add)
-        send(c, "ac%d" % t, [("cnt", t)])
+    def running(t, a, b):
+        carry(a, b, piece[a][2], list(range(1, b - a)), a == 0, True)
+        o, k = within(a, b)
+        mmul(o, T.hi[:, span(a, b, 8, PAD)], T.qq[:], True, True, ["qq"] + keys(a, b, "hi"), [k])
 
-    def blocks(t, j):
+    def early(t, a, b):
+        carry(a, b, 1 - piece[a - 1][2], list(range(b - a, b)), True, False)
+
+    def infected(t, a, b):
+        o, k = within(a, b)
+        bank = ("tb", "ta")[piece[a][2]]
+        ts(T.it[0:8 * (b - a), span(a, a + 1)], o, T[bank][0:8 * (b - a), 64:65], A.subtract, [k, (bank, "c")], [("it", a)],
+           TOP - CAP, A.is_gt)
+
+    def quick(t, a, b, j):
+        assert a == 0 and RUN * b <= CAP
+        o, k = T.cn[0:8 * b, 256:384], ("cn", "in", 0)
+        piece[0] = (0, b, 0)
+        if j:
+            ts(T.it[0:8 * b, 0:RUN], o, float(TH), A.is_ge, [k], [("it", 0)])
+            return
+        for r in range(b):
+            mmul(o, T.zb[:, 16 - 8 * r:16 + 8 * (b - r)], slots(T.xs, r, r + 1, 4), r == 0, r + 1 == b, ["zb", ("x", r)], [k])
+
+    def spread(t, a, b):
+        e, (pa, pb, par) = ebank[a], piece[a]
+        for r in range(a, b):
+            mmul(T[e][:, span(r - a, r - a + 1)], T.ee[0:8 * (pb - pa), span(r - pa, r - pa + 1)],
+                 T.it[0:8 * (pb - pa), span(pa, pa + 1)], False, r + 1 == b, ["ee", ("it", pa)], [(e,)])
+
+    def mask(t, a, b, qn):
+        e = ebank[a]
+        relu(qn, T["win%d" % t][:, span(a, b, RUN, q * P)], T[e][:, span(0, b - a)], [(e,)], keys(a, b, "win", t), -256.0)
+
+    def share(t, a, b):
+        send(T["win%d" % t][:, span(a, b, RUN, q * P)], "al%d_%d" % (t, a), keys(a, b, "win", t))
+
+    def listed(t, j):
         ill = ills[t % 2]
         if j == 0:
-            for o, l, c in ((192, "mb", "cq"), (128, "lt", "cd")):
-                mmul(T.cn[:, o:o + 64], T[l][:], ill[:], True, False, [l] + illk(t), [("cn", o)])
-                mmul(T.cn[:, o:o + 64], T.idn[:], T[c][:], False, True, ["idn", c], [("cn", o)])
-            act(T.rl[:], T.cn[:, 192:256], F.Relu, [("cn", 192)], ["rl"], scale=128.0, bias=-1984.0)
-            act(T.dm[:], T.cn[:, 128:192], F.Copy, [("cn", 128)], ["dm"])
-            return
-        o = T.ta[:, 64:68]
-        mmul(o, T.idn[:], T.c16[:], True, False, ["idn", "c16"], [("ta", "r")])
-        for i in range(16):
-            mmul(o, T.bn[:, 16 - i:144 - i], T.pre[:, i:64:16], False, False, ["bn", "pre", "pre0"], [("ta", "r")])
-        for i in range(16):
-            mmul(o, T.bp[:, 16 - i:144 - i], T.rl[:, i:64:16], False, i == 15, ["bp", "rl"], [("ta", "r")])
-        if right:
-            b = 16 * t + 4 * q
-            ts(T.bo[:], o, T.cnt[:, b:b + 1], A.add, [("ta", "r"), ("cnt", t)], ["bo"], TOP - CAP - LIFT[q], A.add)
+            for i in range(16):
+                mmul(T.cn[:, 128:192], T.bp[:, 16 - i:144 - i], T["win%d" % t][:, q * P + i:(q + 1) * P:16], i == 0, i == 15,
+                     ["bp"] + keys(0, 8, "win", t), [("cn", 128)])
+        elif j == 1:
+            ts(ill[:], T.cn[:, 128:192], float(TH), A.is_ge, [("cn", 128)], [("ill", t % 2)])
+            mmul(T.cn[:, 0:64], T.mb[:], ill[:], True, True, ["mb", ("ill", t % 2)], [("cn", 0)])
         else:
-            ts(T.bo[:], o, TOP - CAP, A.add, [("ta", "r")], ["bo"])
+            scan(tally(t, q, 1, 68), T.cn[:, 0:67], T.m16[:], 0.0, A.add, A.add, ["m16", ("cn", 0), ("cn", 64)], [("pre", t)])
+
+    def counts(t):
+        send(tally(t, q, 64, 66), "ac%d" % t, [("pre", t)])
+
+    def blocks(t, j, qn="V"):
+        ill = ills[t % 2]
+        o = T.ta[:, 128:132]
+        if j == 0:
+            for n, l, k, c in ((192, "mq", "mq", "cq"), (256, "lt", "idn", "cd")):
+                mmul(T.tb[:, n:n + 64], T[k][:], T[c][:], True, False, [k, c], [("tb", n)])
+                mmul(T.tb[:, n:n + 64], T[l][:], ill[:], False, True, [l, ("ill", t % 2)], [("tb", n)])
+        elif j == 1:
+            tt(T.rl[:], tally(t, q, 0, 64), T.tb[:, 192:256], A.min, [("pre", t), "pre0", ("tb", 192)], ["rl"])
+        elif j == 2 and qn == "S":
+            act(T.dm[:], T.tb[:, 256:320], F.Copy, [("tb", 256)], ["dm"])
+        elif j == 2:
+            cpy(T.dm[:], T.tb[:, 256:320], [("tb", 256)], ["dm"])
+        elif j == 3:
+            if right:
+                mmul(o, T.idn[:], tally(t, q, 64, 68), True, False, ["idn", ("pre", t)], [("ta", "r")])
+            for i in range(16):
+                mmul(o, T.bn[:, 16 - i:144 - i], T.rl[:, i:64:16], i == 0 and not right, i == 15, ["bn", "rl"], [("ta", "r")])
+        else:
+            ts(T.bo[:], o, float(P * right), A.add, [("ta", "r")], ["bo"])
+
+    def ground(t):
+        iota(T.bg[:, 0:P], [[0, P]], 1, 0, ["bg"], **small)
 
     def spell(t, j):
         if j == 0:
             cpy(T.bg[:].indirect(T.bo[:]), T.dm[:], ["bo", "dm"], ["bg"])
             return
         seg = T["sw%d" % t][:, q * P:(q + 1) * P]
-        scan(seg, T.up[:], T.bg[:, 0:P], 1.0, A.add, A.min, ["up", "bg"], [("sw", t, "own")])
-        send(seg, "as%d" % t, [("sw", t, "own")])
-        if t < DAYS - 1:
-            iota(T.bg[:, 0:P], [[0, P]], 1, 0, ["bg"], **small)
+        scan(seg, T.up[:], T.bg[:, 0:P], 1.0, A.add, A.min, [("up", 0), ("up", 4), "bg"], [("sw", t, "own")])
 
-    def fade(t, p, qn):
-        relu(qn, slots(T.slot, 16 * CUT[p], 16 * CUT[p + 1], 4), slots(T.xs, 16 * CUT[p], 16 * CUT[p + 1], 4), [("x", p)],
-             [("slot", p, 4)], -8.0)
+    def tell(t):
+        send(T["sw%d" % t][:, q * P:(q + 1) * P], "as%d" % t, [("sw", t, "own")])
+        if t < DAYS - 1:
+            ground(t)
+
+    def fade(t, a, b, qn):
+        relu(qn, slots(T.slot, a, b, 4), slots(T.xs, a, b, 4), keys(a, b, "x"), keys(a, b, "slot", 4), -8.0)
 
     def places(t, j):
-        b = 16 * t
-        rd = [("cnt", t), ("cnt", t, "rem")]
         y = T.sl0[:, 256:512]
+        slope, edge, start, gap = (T.ta[:, n:n + 1] for n in range(240, 244))
         if j == 0:
-            act(T.junk[:], T.cnt[:, b:b + 13:4], F.Copy, rd, [("ka", t), "junk"], scale=1.0 / 2048, accum_out=T.ka[:, t:t + 1])
-            act(T.kb[:, t:t + 1], T.cnt[:, b + 4:b + 5], F.Identity, rd, [("kb", t)], bias=T.cnt[:, b + 8:b + 9])
+            for o, l, a, b in ((240, "idn", 0, 4), (240, "idk", 4, 8), (243, "idn", 2, 3), (243, "idn", 2, 3)):
+                mmul(T.ta[:, o:244], T[l][:], T.cst[:, a:b], a == 0, False, [l, "cst"], [("ta", "k")])
+            terms = [(slope, "idk", r) for r in range(4)] + [(gap, "idn", 1), (gap, "idn", 2), (start, "idn", 0), (edge, "idn", 1)]
+            for n, (o, l, r) in enumerate(terms):
+                mmul(o, T[l][:], tally(t, r, 64, 65), False, n == 7, [l, ("pre", t), ("cnt", t, "rem")], [("ta", "k")])
         elif j == 1:
-            ts(y, T["dd%d" % t][:], T.ka[:, t:t + 1], A.mult, [("dd", t), ("ka", t)] + rd, [("sl0", "y")], T.cnt[:, b:b + 1],
-               A.subtract)
+            ts(y, T["dd%d" % t][:], slope, A.mult, [("dd", t), ("ta", "k")], [("sl0", "y")], start, A.subtract)
         elif j == 2:
-            ts(T.hh[:], y, T.cnt[:, b + 4:b + 5], A.is_le, [("sl0", "y"), ("kb", t)] + rd, ["hh"], T.kb[:, t:t + 1], A.mult)
+            ts(T.hh[:], y, edge, A.is_le, [("sl0", "y"), ("ta", "k")], ["hh"], gap, A.mult)
         elif j == 3:
             tt(T.oi[:], T.hh[:], y, A.subtract, [("sl0", "y"), "hh"], ["oi"])
         else:
             cpy(T["offs%d" % (t % 2)][:], T.oi[:], ["oi"], [("offs", t % 2)])
 
-    def gather(t, p, k, qn):
-        wk = [("win", t, o, n) for o in range(NP) for n in range(len(parts[o]))] + [("win", t, o, "rem") for o in range(NP)]
-        s = T["win%d" % t][:].indirect(T.off[:, 64 * k + CUT[p]:64 * k + CUT[p + 1]])
-        relu(qn, slots(T.slot, 16 * CUT[p], 16 * CUT[p + 1], k), s, wk + [("off", k)], [("slot", p, k)])
+    def gather(t, a, b, k, qn):
+        s = T["win%d" % t][:].indirect(T.off[:, span(a, b, 8, 64 * k)])
+        relu(qn, slots(T.slot, a, b, k), s, keys(0, 8, "win", t) + keys(0, 8, "far", t) + [("off", k)], keys(a, b, "slot", k))
 
-    def newx(t, p):
-        a, b = 80 * CUT[p], 80 * CUT[p + 1]
-        scan(T.xs[:, a:b], T.step[:, a:b], T.slot[:, a:b], 0.0, A.add, A.max,
-             ["step0", "step1", "step4"] + [("slot", p, k) for k in range(5)], [("x", p)])
+    def newx(t, a, b):
+        s = span(a, b, 5 * RUN)
+        scan(T.xs[:, s], T.step[:, s], T.slot[:, s], 0.0, A.add, A.max,
+             keys(0, 5, "step") + [("step", k, o) for k in range(5) for o in (0, 4)] + [n for k in range(5) for n in keys(a, b, "slot", k)], keys(a, b, "x"))
 
-    def result(t, p, qn):
-        relu(qn, T.yo[:, hs[p]], slots(T.xs, 16 * CUT[p], 16 * CUT[p + 1], 4), [("x", p)], [("yo", p)])
-        dma("Y", T.yx[:, hs[p]], T.yo[:, hs[p]], [("yo", p)], [("yx", p)])
+    def result(t, a, b, qn):
+        o, x = T.yo[:, span(a, b)], slots(T.xs, a, b, 4)
+        if qn == "G":
+            emit("G", lambda: g.affine_select(o, x, [[0, RUN * (b - a)]], A.is_equal, 0.0, 0, 0), keys(a, b, "x"), keys(a, b, "yo"))
+        else:
+            relu(qn, o, x, keys(a, b, "x"), keys(a, b, "yo"))
+        dma("Y", T.yx[:, span(a, b)], T.yo[:, span(a, b)], keys(a, b, "yo"), keys(a, b, "yx"))
 
     def slfetch(t, a, b, qn):
-        s = T["sw%d" % t][:].indirect(T["offs%d" % (t % 2)][:, 32 * a:32 * b + 32])
-        relu(qn, T.rsl[:, 512 * a:512 * b + 512], s, [("sw", t, "own"), ("sw", t, "rem"), ("offs", t % 2)],
-             [("rsl", u) for u in range(a, b + 1)])
+        s = T["sw%d" % t][:].indirect(T["offs%d" % (t % 2)][:, span(a, b, 32)])
+        relu(qn, T.rsl[:, span(a, b, 512)], s, [("sw", t, "own"), ("sw", t, "rem"), ("offs", t % 2)], keys(a, b, "rsl"))
+
+    sums = {}
+
+    def opened(t, a, b):
+        bank = ("ht", "e0", "sl1", "sl0")[a]
+        mmul(T[bank][:, span(0, b - a, 64)], T.w2[:], T.top[0:64, span(0, b - a, 64)], True, False, keys(0, 2, "w2") + ["top"],
+             [(bank,)])
+        for k in range(a, b):
+            sums[k] = (bank, a, b)
 
     def hits(t, k):
-        o = T.ht[:, 64 * k:64 * k + 64]
-        mmul(o, T.ineg[:], ills[t % 2][:], True, False, ["ineg"] + illk(t), [("ht", k)])
+        bank, a, b = sums[k]
+        o = T[bank][:, span(k - a, k - a + 1, 64)]
+        mmul(o, T.ineg[:], ills[t % 2][:], False, False, ["ineg", ("ill", t % 2)], [(bank,)])
         for i in range(16):
-            mmul(o, T.bp[:, 16 - i:144 - i], slots(T.slot, i, P, k, 16), False, i == 15,
-                 ["bp"] + [("slot", p, k) for p in range(NP)], [("ht", k)])
-
-    def ks(a, b, base=0):
-        return slice(base + 64 * a, base + 64 * b + 64)
-
-    def keys(a, b, *name):
-        return [name + (k,) for k in range(a, b + 1)]
-
-    SB = ("sl0", "e0", "sl1", "e1")
+            mmul(o, T.hb[:, 16 - i:144 - i], slots(T.slot, 0, 8, k, i, 16), False, False, ["hb"] + keys(0, 8, "slot", k), [(bank,)])
 
     def slsum(t, a, b):
-        l = ("idn", "id2", "id3", "id4")[t]
-        o = T[SB[a]][:, ks(0, b - a)]
-        mmul(o, T[l][:], T.sg[:, ks(a, b)], True, False, [l] + keys(a, b, "sg"), [(SB[a], "s")])
+        bank, o, end = sums[a]
         for i in range(16):
-            mmul(o, T.cp[:, 16 - i:144 - i], T.rsl[:, 1024 * a + i:1024 * (b + 1):16], False, i == 15,
-                 ["cp"] + [("rsl", u) for u in range(2 * a, 2 * b + 2)], [(SB[a], "s")])
-
-    def struck(t, a, b):
-        act(T.sg[:, ks(a, b)], T.ht[:, ks(a, b)], F.Sign, keys(a, b, "ht"), keys(a, b, "sg"), bias=-float(TH) / 2)
-
-    def keep(t, a, b):
-        tt(T.lk[:, ks(a, b)], T.ht[:, ks(a, b, 256)], T.sg[:, ks(a, b)], A.subtract, keys(a, b, "ht", "ll") + keys(a, b, "sg"),
-           keys(a, b, "lk"))
+            mmul(T[bank][:, span(a - o, b - o, 64)], T.cp[:, 16 - i:144 - i], T.rsl[:, P * a + i:P * b:16], False,
+                 i == 15 and b == end, ["cp"] + keys(2 * a, 2 * b, "rsl"), [(bank,)])
 
     def renew(t, a, b):
-        new = T[SB[a]][:, ks(0, b - a)]
-        if t < DAYS - 1:
-            tt(T.ht[:, ks(a, b, 256)], T.lk[:, ks(a, b)], new, A.max, keys(a, b, "lk") + [(SB[a], "s")], keys(a, b, "ht", "ll"))
-        else:
-            tt(T.lk[:, ks(a, b)], T.lk[:, ks(a, b)], new, A.max, keys(a, b, "lk") + [(SB[a], "s")], keys(a, b, "lk"))
+        s, bank = span(a, b, 64), sums[a][0]
+        tt(T.ni[:, s], T.ni[:, s], T[bank][:, span(0, b - a, 64)], A.max, keys(a, b, "ni") + [(bank,)], keys(a, b, "ni"))
+
+    def strip(t, a, b):
+        s = span(a, b, 64)
+        ts(T.ni[:, s], T.ni[:, s], 4 * P - 1, A.bitwise_and, keys(a, b, "ni"), keys(a, b, "ni"))
 
     def offnew(t, a, b):
+        s = span(a, b, 64)
         if t < DAYS - 1:
-            ts(T.off[:, ks(a, b)], T.ht[:, ks(a, b, 256)], C0 - t - 1, A.add, keys(a, b, "ht", "ll"), keys(a, b, "off"), SH, A.mult)
+            cpy(T.off[:, s], T.ni[:, s], keys(a, b, "ni"), keys(a, b, "off"))
         else:
-            ts(T.no[:, ks(a, b)], T.lk[:, ks(a, b)], C0 - t - 1, A.add, keys(a, b, "lk"), keys(a, b, "no"), SH, A.mult)
-            dma("Y", T.ynb[:, ks(a, b)], T.no[:, ks(a, b)], keys(a, b, "no"), keys(a, b, "ynb"))
+            cpy(T.no[:, s], T.ni[:, s], keys(a, b, "ni"), keys(a, b, "no"))
+            dma("Y", T.ynb[:, s], T.no[:, s], keys(a, b, "no"), keys(a, b, "ynb"))
 
     last = T.r16[:, 15:16]
 
     def number():
         ts(T.rw[:], T.ri[:], -1.0, A.mult, ["ri"], ["rw"])
         dma("Y", T.rneg[0:8, :], T.rw[:], ["rw"], ["rneg"])
-        ts(T.pmi[:], T.t1[:, 0:1], 15, A.bitwise_and, ["t1"], ["pmi"])
-        tt(T.lt[:], T.idn[:], T.su[:], A.subtract, ["idn", "su"], ["lt"])
-        cpy(T.col[:, 0:1], T.pmi[:], ["pmi"], ["col0"])
-        fill(T.lt[:, 15:128:16], 0.0, ["lt"])
 
-    def offsets():
-        cpy(T.off[:], T.ni[:], ["ni"], keys(0, 3, "off"))
+    short = [
+        lambda: ts(T.pre[:, 80 * q::320], T.top[:, 0:DAYS], 0.0, A.mult, ["top"], ["pre0"]),
+        lambda: fill(T.m16[:], -16.0, ["m16"]),
+        lambda: fill(T.cn[:, 64:67], 16.0, [("cn", 64)]),
+        lambda: ts(T.pmi[:], T.t1[:, 0:1], 15, A.bitwise_and, ["t1"], ["pmi"]),
+        lambda: cpy(T.col[:, 0:1], T.pmi[:], ["pmi"], ["col0"]),
+        lambda: ts(T.col[:, 1:2], last, (15 + (255.0 - 64 * q) / 256) / 256, A.mult, ["r16", "col0"], ["col1"], T.col[:, 0:1],
+                   A.subtract),
+        lambda: emit("G", lambda: g.affine_select(T.lt[:], T.mb[:], [[1, 128]], A.is_ge, 0.0, 0, -1), ["mb"], ["lt"]),
+        lambda: fill(T.lt[:, 15:128:16], 0.0, ["lt"]),
+        lambda: iota(T.cc[:], [[1, 64]], 0, 0, ["cc"], **small),
+        lambda: ts(T.cq[:], T.cc[:], -2016.0, A.add, ["cc"], ["cq"], 1.0 / 2048, A.mult),
+        lambda: iota(T.csi[:, 0:4], [[2048, 2], [-2048, 2]], 0, 0, [("csi", 0)]),
+        lambda: iota(T.csi[:, 4:8], [[-2047, 2], [2047, 2]], 0, 0, [("csi", 1)]),
+        lambda: ts(T.cst[:], T.csi[:], 0.5, A.mult, keys(0, 2, "csi"), ["cst"]),
+        lambda: fill(T.w2[0:32, :], 255 * 16 / 32, [("w2", 0)]),
+        lambda: fill(T.w2[32:64, :], -512 * 4096 / 32, [("w2", 1)]),
+    ]
 
-    def one():
-        ts(T.col[:, 1:2], last, (15 + (255.0 - 64 * q) / 256) / 256, A.mult, ["r16", "col0"], ["col1"], T.col[:, 0:1], A.subtract)
-        ts(T.c16[:], T.m16[:], T.col[:, 0:1], A.add, ["m16", "col0"], ["c16"], 16.0, A.mult)
+    def bit(t, a, b):
+        short[10 * a + b]()
 
     def blk():
         act(T.col[:, 2:3], last, F.Copy, ["r16"], ["col2"], scale=-1.0 / 65536)
-        act(T.cq[:], T.cc[:], F.Copy, ["cc"], ["cq"], scale=1.0 / 256)
-        act(T.col[:, 3:4], last, F.Copy, ["r16"], ["col3"], scale=-1.0 / 256, bias=1.0)
-        act(T.cd[:], T.cc[:], F.Identity, ["cc", "col1", "col2"], ["cd"], scale=T.col[:, 2:3], bias=T.col[:, 1:2])
+        act(T.mq[:], T.mb[:], F.Copy, ["mb"], ["mq"], scale=-4096.0)
         act(T.bn[:], T.bp[:], F.Copy, ["bp"], ["bn"], scale=-1.0 / 16)
-        act(T.up[:], T.bg[:, 0:P], F.Copy, ["bg", "col3"], ["up"], scale=T.col[:, 3:4])
+        act(T.cd[:], T.cc[:], F.Identity, ["cc", "col1", "col2"], ["cd"], scale=T.col[:, 2:3], bias=T.col[:, 1:2])
+
+    def rise():
+        act(T.col[:, 3:4], last, F.Copy, ["r16"], ["col3"], scale=-1.0 / 256, bias=1.0)
+        for a in (0, 4):
+            act(T.up[:, span(a, a + 4)], T.ht[:], F.Identity, [("ht",), "col3"], [("up", a)], scale=0.0, bias=T.col[:, 3:4])
 
     def resist():
         for n in (0, 1):
-            e = "e%d" % n
-            mmul(T[e][:], T.er[:], T.rneg[:, 512 * n:512 * n + 512], True, True, ["er", "rneg"], [(e,)])
-            act(slots(T.step, 512 * n, 512 * n + 512, 4), T[e][:], F.Copy, [(e,)], ["step4"])
+            e = "sl%d" % n
+            mmul(T[e][:], T.er[:], T.rneg[:, span(n, n + 1, 512)], True, True, ["er", "rneg"], [(e,)])
+            act(slots(T.step, 4 * n, 4 * n + 4, 4), T[e][:], F.Copy, [(e,)], [("step", 4, 4 * n)])
 
-    def steps():
-        fill(slots(T.step, 0, P, 0), -1024.0, ["step0"])
-        fill(slots(T.step, 0, P, 1), 0.0, ["step1"])
-        for k in (2, 3):
-            act(slots(T.step, 0, P, k), T.up[:], F.Copy, ["up"], ["step4"], scale=0.0)
+    def steps(t, k, qn):
+        if qn == "V":
+            fill(slots(T.step, 0, 8, k), 0.0 if k else -1024.0, [("step", k)])
+        else:
+            for a in (0, 4):
+                act(slots(T.step, a, a + 4, k), T.ht[:], F.Copy, [("ht",)], [("step", k, a)], scale=0.0, bias=0.0 if k else -1024.0)
 
     def misc():
-        act(T.col[:, 4:5], last, F.Copy, ["r16"], ["col4"], scale=-(0.5 + 1 / SH) / 256, bias=1 / SH)
-        act(T.ineg[:], T.idn[:], F.Copy, ["idn"], ["ineg"], scale=-SH)
+        act(T.col[:, 4:5], last, F.Copy, ["r16"], ["col4"], scale=-4097.0 / 256, bias=1.0)
+        act(T.ineg[:], T.idn[:], F.Copy, ["idn"], ["ineg"], scale=-2.0 ** 25)
+        act(T.hb[:], T.bp[:], F.Copy, ["bp"], ["hb"], scale=4096.0)
         act(T.cp[:], T.bp[:], F.Copy, ["bp", "col4"], ["cp"], scale=T.col[:, 4:5])
-        for n in (2, 3, 4):
-            act(T["id%d" % n][:], T.idn[:], F.Copy, ["idn"], ["id%d" % n], scale=float(n))
-        ts(T.ht[:, 256:512], T.ni[:], 1.0 / SH, A.mult, ["ni"], keys(0, 3, "ht", "ll"), -C0, A.add)
+        act(T.idk[:], T.idn[:], F.Copy, ["idn"], ["idk"], scale=1.0 / 2048)
 
     def draws(t, n):
         ts(T["dd%d" % n][:], T.dd0[:], STEP * n, A.add, [("dd", 0)], [("dd", n)])
@@ -470,11 +515,11 @@ def rank_program(g, core, T, topo):
     def wrap(t, n):
         ts(T["dd%d" % n][:], T["dd%d" % n][:], M2, A.bitwise_and, [("dd", n)], [("dd", n)])
 
-    once = {"num": number, "off": offsets, "one": one, "blk": blk, "res": resist, "slots": steps, "misc": misc}
-    flags = {"T": total, "a": high, "F": running, "v": counted, "i": infected, "s": spread, "m": mask, "C": counts,
-             "Z": blocks, "M": spell, "D": fade}
-    day = {"g": gather, "c": newx, "y": result, "k": slfetch, "S": slsum, "u": struck, "K": keep, "R": renew, "O": offnew,
-           "h": hits, "p": places, "d": draws, "w": wrap}
+    once = {"num": number, "blk": blk, "rise": rise, "res": resist, "misc": misc}
+    flags = {"x": widen, "T": total, "l": lift, "a": high, "F": running, "E": early, "i": infected, "s": spread, "m": mask,
+             "W": share, "L": listed, "C": counts, "Z": blocks, "M": spell, "N": tell, "D": fade, "B": ground, "q": quick}
+    day = {"g": gather, "c": newx, "y": result, "k": slfetch, "S": slsum, "H": opened, "A": strip, "R": renew, "O": offnew,
+           "h": hits, "p": places, "d": draws, "w": wrap, "z": steps, "b": bit}
 
     def run(t, order):
         for n in order.split():
@@ -491,7 +536,7 @@ def rank_program(g, core, T, topo):
         run(t, DAY)
     run(DAYS - 1, LAST)
 
-    sync_to("G", [lastw[k] for k in keys(0, 3, "ynb")] + [lastw[("yx", p)] for p in range(NP)])
+    sync_to("G", [lastw[k] for k in keys(0, 4, "ynb") + keys(0, 8, "yx")])
     for k in ("V", "S", "P", "G"):
         g.wait_ge(T.sem[psem[k]], done[k])
     g.wait_ge(T.sem.sent, nsent[0])

@@ -5,17 +5,17 @@ DAYS, P, CAP, TH, STEP, M2 = 4, 1024, 384, 1200, 77, 2047
 RUN = 128
 TOP = 2048.0
 BG = 3456
-WIDE = 48
+WIDE = 56
 PAD = WIDE - 8
-LOAD = "02Y rS 25S 58Y nY dS"
-FIRST = """z1S z2S b11 b10 b08 b06 x02 q020 q021 T02 l02 a02 s02 E28 num m02S W02 x25 l25 x58 T28 b03 l58 a28 z3S F28 b09 i28 s25
- s58 b12 b02 m25S m58V W28 D04V b14 rise b07 L0 D48S d3 O04 b01 b04 b05 blk res L1 d1 b13 b00 misc L2 C B w3 d2 w2 Z0 w1 z0V Z1
- Z3 Z2V Z5 M0 M1 N"""
-DAY = """H23 g030V g031S g033V p0 p1 g032S H02 H34 c03 q030 g363S g360S g362V T03 g361S l03 q031 g683S g682S s03 m03S W03 h3 c36
- a03 g680S p2 T36 g681S l36 E36 a36 p3 F36 i36 p4 h0 s36 h1 k01S c68 m36V W36 T68 k12S E68 a68 F68 i68 l68 s68 D04V m68V W68 h2
- k34S L0 k23V L1 D48V k45S Z0 L2 C S01 Z2V Z1 k56V Z3 S12 Z5 M0 S23 M1 N R02 k78S R23 k67S S34 A02 O02 R34 A24 O24"""
-LAST = """g040V p0 p1 g481S g042V p2 H01 g480S H12 g041S g043S g482S p3 c04 p4 g483S c48 k01V h0 k12S H34 k56V h3 y04G h1 H23 h2
- k45S S01 k23S S23 k67V R23 A23 R01 k34S S12 R12 A02 y48G O23 O02 k78S S34 R34 A34 O34"""
+LOAD = "01Y rS 14S 48Y nY dS"
+FIRST = """x01 z2S b02 l01 b13 q010 q011 T01 x14 z3S a01 x48 b00 s01 num m01S b08 b09 l14 b15 b03 T18 a18 E18 d3 b10 F18 l48 i18
+ b06 W01 d2 b01 b04 d1 rise D04S b05 s48 s14 m48S m14V W18 L0 blk D48V z1V b07 misc L1 z0V Z0 res L2 Z2V Z1 B b14 w1 w3 Z3 O04 C
+ Z5 b11 w2 M0 b12 M1 N"""
+DAY = """H02 g031S g030V H34 g032S g360S p0 g361S g033V p1 g362S c03 q030 g683S T03 l03 g363V h3 q031 s03 g682S c36 p2 g681S T36
+ H23 g680S a03 l36 a36 c68 E36 F36 m03S W03 i36 D04S h0 T68 p3 s36 m36S W36 E68 l68 a68 p4 F68 i68 h1 k01S k34V k12V k23V s68
+ m68S W68 h2 L0 S01 L1 Z0 S12 D48V L2 C k45S Z1 Z3 R02 A02 k78S Z5 k56S S23 Z2S O02 M0 R23 M1 N k67S S34 R34 A24 O24"""
+LAST = """p0 p1 g040S g480S g481S g041S j0 j1 p2 g043V g483S g042S p3 g482V u02 J0 p4 j2 c48 k01S k12S J1 c04 k45V j3 S01 k34V
+ k56S k67V u24 y48G J2 S23 k23S k78S K24 S12 K02 y04G r2 r0 J3 S34 r1 o03Y r3 o34Y"""
 
 
 def _sb(dtype, *names, cols, rows=128):
@@ -42,7 +42,8 @@ SCRATCH.update(_sb("bfloat16", "ee", "big", cols=16 * WIDE, rows=WIDE))
 SCRATCH.update(_sb("bfloat16", "it", cols=P, rows=WIDE))
 SCRATCH.update(_sb("bfloat16", "hi", cols=PAD + 64))
 SCRATCH.update(_sb("bfloat16", "zb", cols=40))
-SCRATCH.update(_sb("bfloat16", "w2", cols=128, rows=64))
+SCRATCH.update(_sb("bfloat16", "w2", cols=128, rows=96))
+SCRATCH.update(_sb("bfloat16", "sg", cols=256))
 SCRATCH.update(_sb("bfloat16", "bp", "cp", "bn", "hb", cols=144))
 SCRATCH.update(_sb("bfloat16", "mb", "mq", "idn", "idk", "ineg", "su1", "i2", "lt", "qq", "top", cols=128))
 SCRATCH.update(_sb("bfloat16", "ill0", "ill1", "rw", "cc", "cd", "dm", cols=64))
@@ -151,6 +152,9 @@ def rank_program(g, core, T, topo):
         queue[qn].dma_start(out, in_).then_inc(T.sem[s], 16)
         record((s, 16, dict(known[qn]), None), reads, writes)
 
+    def keys(a, b, *name):
+        return [name + (k,) for k in range(a, b)]
+
     def send(ap, sem, reads):
         deps("G", reads, [], False)
         tr = []
@@ -160,9 +164,6 @@ def rank_program(g, core, T, topo):
                                         dma_engine_mask=sum(1 << x for x in es), remote_sem=T.sem[sem]))
             nsent[0] += len(es)
         g.remote_dma_fused(tr, local_sem=T.sem.sent)
-
-    def keys(a, b, *name):
-        return [name + (k,) for k in range(a, b)]
 
     arrive = sum(len(eng[c][core]) for c in cores if c != core)
     for t in range(DAYS):
@@ -319,6 +320,9 @@ def rank_program(g, core, T, topo):
     def share(t, a, b):
         send(T["win%d" % t][:, span(a, b, RUN, q * P)], "al%d_%d" % (t, a), keys(a, b, "win", t))
 
+    def counts(t):
+        send(tally(t, q, 64, 66), "ac%d" % t, [("pre", t)])
+
     def listed(t, j):
         ill = ills[t % 2]
         if j == 0:
@@ -330,9 +334,6 @@ def rank_program(g, core, T, topo):
             mmul(T.cn[:, 0:64], T.mb[:], ill[:], True, True, ["mb", ("ill", t % 2)], [("cn", 0)])
         else:
             scan(tally(t, q, 1, 68), T.cn[:, 0:67], T.m16[:], 0.0, A.add, A.add, ["m16", ("cn", 0), ("cn", 64)], [("pre", t)])
-
-    def counts(t):
-        send(tally(t, q, 64, 66), "ac%d" % t, [("pre", t)])
 
     def blocks(t, j, qn="V"):
         ill = ills[t % 2]
@@ -415,8 +416,8 @@ def rank_program(g, core, T, topo):
     sums = {}
 
     def opened(t, a, b):
-        bank = ("ht", "e0", "sl1", "sl0")[a]
-        mmul(T[bank][:, span(0, b - a, 64)], T.w2[:], T.top[0:64, span(0, b - a, 64)], True, False, keys(0, 2, "w2") + ["top"],
+        bank = {0: "ht", 2: "sl1", 3: "sl0"}[a]
+        mmul(T[bank][:, span(0, b - a, 64)], T.w2[0:64, :], T.top[0:64, span(0, b - a, 64)], True, False, keys(0, 2, "w2") + ["top"],
              [(bank,)])
         for k in range(a, b):
             sums[k] = (bank, a, b)
@@ -444,11 +445,37 @@ def rank_program(g, core, T, topo):
 
     def offnew(t, a, b):
         s = span(a, b, 64)
-        if t < DAYS - 1:
-            cpy(T.off[:, s], T.ni[:, s], keys(a, b, "ni"), keys(a, b, "off"))
-        else:
-            cpy(T.no[:, s], T.ni[:, s], keys(a, b, "ni"), keys(a, b, "no"))
-            dma("Y", T.ynb[:, s], T.no[:, s], keys(a, b, "no"), keys(a, b, "ynb"))
+        cpy(T.off[:, s], T.ni[:, s], keys(a, b, "ni"), keys(a, b, "off"))
+
+    def closed(t, k):
+        o = T.ht[:, span(k, k + 1, 64)]
+        mmul(o, T.ineg[:], ills[t % 2][:], True, False, ["ineg", ("ill", t % 2)], [("ht", k)])
+        for i in range(16):
+            mmul(o, T.hb[:, 16 - i:144 - i], slots(T.slot, 0, 8, k, i, 16), False, i == 15, ["hb"] + keys(0, 8, "slot", k), [("ht", k)])
+
+    def struck(t, a, b):
+        s = span(a, b, 64)
+        act(T.sg[:, s], T.ht[:, s], F.Sign, keys(a, b, "ht"), keys(a, b, "sg"), bias=-512.0 * 4096)
+        o = T.cn[:, s]
+        mmul(o, T.i2[:], T.top[:, span(0, b - a, 64)], True, False, ["i2", "top"], keys(a, b, "cn", "k"))
+        mmul(o, T.i2[:], T.sg[:, s], False, True, ["i2"] + keys(a, b, "sg"), keys(a, b, "cn", "k"))
+
+    def keep(t, a, b):
+        s = span(a, b, 64)
+        tt(T.no[:, s], T.ni[:, s], T.cn[:, s], A.subtract, keys(a, b, "ni") + keys(a, b, "cn", "k"), keys(a, b, "no"))
+
+    def drawn(t, k):
+        bank = ("ta", "tb", "e0", "e1")[k]
+        mmul(T[bank][:, 0:64], T.w2[64:96, :], T.top[64:96, 0:64], True, False, [("w2", 2), "top"], [(bank,)])
+        mmul(T[bank][:, 0:64], T.i2[:], T.sg[:, span(k, k + 1, 64)], False, False, ["i2", ("sg", k)], [(bank,)])
+        sums[k] = (bank, k, k + 1)
+
+    def final(t, k):
+        s, bank = span(k, k + 1, 64), sums[k][0]
+        tt(T.no[:, s], T.no[:, s], T[bank][:, 0:64], A.max, [("no", k), (bank,)], [("no", k)])
+
+    def store(t, a, b, qn):
+        dma(qn, T.ynb[:, span(a, b, 64)], T.no[:, span(a, b, 64)], keys(a, b, "no"), keys(a, b, "ynb"))
 
     last = T.r16[:, 15:16]
 
@@ -473,6 +500,7 @@ def rank_program(g, core, T, topo):
         lambda: ts(T.cst[:], T.csi[:], 0.5, A.mult, keys(0, 2, "csi"), ["cst"]),
         lambda: fill(T.w2[0:32, :], 255 * 16 / 32, [("w2", 0)]),
         lambda: fill(T.w2[32:64, :], -512 * 4096 / 32, [("w2", 1)]),
+        lambda: fill(T.w2[64:96, :], (255 * 16 - 2048) / 32, [("w2", 2)]),
     ]
 
     def bit(t, a, b):
@@ -517,9 +545,10 @@ def rank_program(g, core, T, topo):
 
     once = {"num": number, "blk": blk, "rise": rise, "res": resist, "misc": misc}
     flags = {"x": widen, "T": total, "l": lift, "a": high, "F": running, "E": early, "i": infected, "s": spread, "m": mask,
-             "W": share, "L": listed, "C": counts, "Z": blocks, "M": spell, "N": tell, "D": fade, "B": ground, "q": quick}
+             "W": share, "C": counts, "N": tell, "L": listed, "Z": blocks, "M": spell, "D": fade, "B": ground, "q": quick}
     day = {"g": gather, "c": newx, "y": result, "k": slfetch, "S": slsum, "H": opened, "A": strip, "R": renew, "O": offnew,
-           "h": hits, "p": places, "d": draws, "w": wrap, "z": steps, "b": bit}
+           "h": hits, "p": places, "d": draws, "w": wrap, "z": steps, "b": bit,
+           "j": closed, "u": struck, "K": keep, "J": drawn, "r": final, "o": store}
 
     def run(t, order):
         for n in order.split():
@@ -531,10 +560,8 @@ def rank_program(g, core, T, topo):
             else:
                 day[n[0]](t, *a)
 
-    run(-1, FIRST)
-    for t in range(DAYS - 1):
-        run(t, DAY)
-    run(DAYS - 1, LAST)
+    for t, order in enumerate((FIRST, DAY, DAY, DAY, LAST)):
+        run(t - 1, order)
 
     sync_to("G", [lastw[k] for k in keys(0, 4, "ynb") + keys(0, 8, "yx")])
     for k in ("V", "S", "P", "G"):

from concourse.bass import DstId, RemoteDMATransfer
from concourse.mybir import AluOpType as A, ActivationFunctionType as F

DAYS, P, CAP, TH, STEP, M2 = 4, 1024, 384, 1200, 77, 2047
RUN = 128
TOP = 2048.0
BG = 3456
WIDE = 56
PAD = WIDE - 8
LOAD = "01Y rS 14S 48Y nY dS"
FIRST = """x01 z2S b02 l01 b13 q010 q011 T01 x14 z3S a01 x48 b00 s01 num m01S b08 b09 l14 b15 b03 T18 a18 E18 d3 b10 F18 l48 i18
 b06 W01 d2 b01 b04 d1 rise D04S b05 s48 s14 m48S m14V W18 L0 blk D48V z1V b07 misc L1 z0V Z0 res L2 Z2V Z1 B b14 w1 w3 Z3 O04 C
 Z5 b11 w2 M0 b12 M1 N"""
DAY = """H02 g031S g030V H34 g032S g360S p0 g361S g033V p1 g362S c03 q030 g683S T03 l03 g363V h3 q031 s03 g682S c36 p2 g681S T36
 H23 g680S a03 l36 a36 c68 E36 F36 m03S W03 i36 D04S h0 T68 p3 s36 m36S W36 E68 l68 a68 p4 F68 i68 h1 k01S k34V k12V k23V s68
 m68S W68 h2 L0 S01 L1 Z0 S12 D48V L2 C k45S Z1 Z3 R02 A02 k78S Z5 k56S S23 Z2S O02 M0 R23 M1 N k67S S34 R34 A24 O24"""
LAST = """p0 p1 g040S g480S g481S g041S j0 j1 p2 g043V g483S g042S p3 g482V u02 J0 p4 j2 c48 k01S k12S J1 c04 k45V j3 S01 k34V
 k56S k67V u24 y48G J2 S23 k23S k78S K24 S12 K02 y04G r2 r0 J3 S34 r1 o03Y r3 o34Y"""


def _sb(dtype, *names, cols, rows=128):
    return {n: ("sbuf", [rows, cols], dtype) for n in names}


SCRATCH = {}
SCRATCH.update(_sb("int32", "xi", cols=P))
SCRATCH.update(_sb("int32", "ni", "dd0", "oi", "dd1", "dd2", "dd3", cols=256))
SCRATCH.update(_sb("int32", "t1", "t2", "t2s", cols=128))
SCRATCH.update(_sb("int32", "ri", cols=64))
SCRATCH.update(_sb("int32", "t3", cols=16))
SCRATCH.update(_sb("int32", "pmi", cols=1))
SCRATCH.update(_sb("uint16", "off", "offs0", "offs1", cols=256))
SCRATCH.update(_sb("uint16", "bo", cols=4))
SCRATCH.update(_sb("bfloat16", "slot", "xs", "step", cols=5 * P))
SCRATCH.update(_sb("bfloat16", "rsl", cols=4 * P))
SCRATCH.update(_sb("bfloat16", *["win%d" % _t for _t in range(DAYS)], *["sw%d" % _t for _t in range(DAYS)], cols=4 * P))
SCRATCH.update(_sb("bfloat16", "bg", cols=BG))
SCRATCH.update(_sb("bfloat16", "up", cols=P))
SCRATCH.update(_sb("bfloat16", "rneg", cols=P, rows=8))
SCRATCH.update(_sb("bfloat16", "er", cols=128, rows=8))
SCRATCH.update(_sb("bfloat16", "ee", "big", cols=16 * WIDE, rows=WIDE))
SCRATCH.update(_sb("bfloat16", "it", cols=P, rows=WIDE))
SCRATCH.update(_sb("bfloat16", "hi", cols=PAD + 64))
SCRATCH.update(_sb("bfloat16", "zb", cols=40))
SCRATCH.update(_sb("bfloat16", "w2", cols=128, rows=96))
SCRATCH.update(_sb("bfloat16", "sg", cols=256))
SCRATCH.update(_sb("bfloat16", "bp", "cp", "bn", "hb", cols=144))
SCRATCH.update(_sb("bfloat16", "mb", "mq", "idn", "idk", "ineg", "su1", "i2", "lt", "qq", "top", cols=128))
SCRATCH.update(_sb("bfloat16", "ill0", "ill1", "rw", "cc", "cd", "dm", cols=64))
SCRATCH.update(_sb("bfloat16", "m16", cols=67))
SCRATCH.update(_sb("float16", "cq", "rl", cols=64))
SCRATCH.update(_sb("float16", "cst", cols=8))
SCRATCH.update(_sb("int32", "csi", cols=8))
SCRATCH.update(_sb("float16", "pre", cols=320 * DAYS))
SCRATCH.update(_sb("float32", "yo", cols=P))
SCRATCH.update(_sb("float32", "no", "hh", cols=256))
SCRATCH.update(_sb("float32", "r16", cols=16))
SCRATCH.update(_sb("float32", "col", cols=8))
BANKS = ("ta", "tb", "cn", "e0", "e1", "ht", "sl0", "sl1")
for _b in BANKS:
    SCRATCH[_b] = ("psum", [128, 512], "float32")
SEMAPHORES = ["pv", "ps", "pp", "pg", "sent"] + ["dm%d" % i for i in range(24)]
SEMAPHORES += ["al%d_%d" % (t, a) for t in range(DAYS) for a in range(8)]
SEMAPHORES += [k + "%d" % t for k in ("ac", "as") for t in range(DAYS)]


def plan(topo, cores, src):
    far = [d for d in cores if d != src and topo.chip(d) != topo.chip(src)]
    near = [d for d in cores if d != src and topo.chip(d) == topo.chip(src)]
    e = {}
    used = []
    for n, d in enumerate(far):
        es = topo.engines(src, d)
        w = len(es) // len(far)
        e[d] = es[n * w:(n + 1) * w]
        used += e[d]
    for n, d in enumerate(near):
        es = [x for x in topo.engines(src, d) if x not in used][::2]
        w = len(es) // len(near)
        e[d] = es[n * w:(n + 1) * w]
    return e


def rank_program(g, core, T, topo):
    q = T.rank_of(core)
    if q is None:
        return
    cores = list(T.cores)
    right = q % 2 == 0
    eng = {c: plan(topo, cores, c) for c in cores}
    queue = {"V": g.vector, "S": g.scalar, "P": g.tensor, "G": g, "Y": g.sync}
    psem = {"V": "pv", "S": "ps", "P": "pp", "G": "pg"}
    done = {k: 0 for k in queue}
    known = {k: {} for k in queue}
    lastw, readers = {}, {}
    visit = {b: {} for b in BANKS}
    ndma = [0]
    nsent = [0]

    def sync_to(qn, toks):
        need = {}
        for t in toks:
            if known[qn].get(t[0], 0) < t[1]:
                if t[1] > need.get(t[0], (0,))[0]:
                    need[t[0]] = (t[1], t)
        for s in sorted(need):
            v, t = need[s]
            if any(o != s and need[o][1][2].get(s, 0) >= v for o in need):
                continue
            queue[qn].wait_ge(T.sem[s], v)
        for s in need:
            v, t = need[s]
            for k2, v2 in t[2].items():
                if known[qn].get(k2, 0) < v2:
                    known[qn][k2] = v2
            if known[qn].get(s, 0) < v:
                known[qn][s] = v

    def banks(keys):
        return {k[0] for k in keys if isinstance(k, tuple) and k[0] in visit}

    def deps(qn, reads, writes, accum):
        toks = [lastw[k] for k in reads if k in lastw]
        for k in writes:
            if k in lastw and not (accum and lastw[k][3] == qn):
                toks.append(lastw[k])
            toks += readers.get(k, [])
        for b in banks(reads + writes):
            toks += [t for o, t in visit[b].items() if o != qn]
        sync_to(qn, toks)

    def record(tok, reads, writes):
        for k in reads:
            readers.setdefault(k, []).append(tok)
        for k in writes:
            lastw[k] = tok
            readers[k] = []
        for b in banks(reads + writes):
            visit[b][tok[3]] = tok

    def emit(qn, fn, reads, writes, accum=False):
        deps(qn, reads, writes, accum)
        s = psem[qn]
        fn().then_inc(T.sem[s], 1)
        done[qn] += 1
        record((s, done[qn], dict(known[qn]), qn), reads, writes)

    def dma(qn, out, in_, reads, writes):
        deps(qn, reads, writes, False)
        s = "dm%d" % ndma[0]
        ndma[0] += 1
        queue[qn].dma_start(out, in_).then_inc(T.sem[s], 16)
        record((s, 16, dict(known[qn]), None), reads, writes)

    def keys(a, b, *name):
        return [name + (k,) for k in range(a, b)]

    def send(ap, sem, reads):
        deps("G", reads, [], False)
        tr = []
        for d, es in eng[core].items():
            rid, pid, se = topo.addr(d)
            tr.append(RemoteDMATransfer(src=ap, dst=ap, dst_ids=[DstId(rid=rid, pnc=pid)],
                                        dma_engine_mask=sum(1 << x for x in es), remote_sem=T.sem[sem]))
            nsent[0] += len(es)
        g.remote_dma_fused(tr, local_sem=T.sem.sent)

    arrive = sum(len(eng[c][core]) for c in cores if c != core)
    for t in range(DAYS):
        for n in (DAY if t else FIRST).split():
            if n[0] == "W":
                for k in keys(int(n[1]), int(n[2]), "far", t):
                    lastw[k] = ("al%d_%s" % (t, n[1]), arrive, {}, None)
        lastw[("cnt", t, "rem")] = ("ac%d" % t, arrive, {}, None)
        lastw[("sw", t, "rem")] = ("as%d" % t, arrive, {}, None)

    def ts(out, in0, s1, op0, r, w, s2=None, op1=None):
        if op1 is None:
            emit("V", lambda: g.vector.tensor_scalar(out, in0, s1, None, op0), r, w)
        else:
            emit("V", lambda: g.vector.tensor_scalar(out, in0, s1, s2, op0, op1), r, w)

    def tt(out, a, b, op, r, w):
        emit("V", lambda: g.vector.tensor_tensor(out, a, b, op), r, w)

    def cpy(out, a, r, w):
        emit("V", lambda: g.vector.tensor_copy(out, a), r, w)

    def fill(out, c, w):
        emit("V", lambda: g.vector.memset(out, c), [], w)

    def scan(out, d0, d1, init, op0, op1, r, w):
        emit("V", lambda: g.vector.tensor_tensor_scan(out, d0, d1, init, op0, op1), r, w)

    def mmul(out, l, rhs, start, stop, r, w):
        emit("P", lambda: g.tensor.matmul(out, l, rhs, start, stop), r, w, accum=not start)

    def act(out, a, f, r, w, **kw):
        emit("S", lambda: g.scalar.activation(out, a, f, **kw), r, w)

    def iota(out, pattern, base, mult, w, **kw):
        emit("G", lambda: g.iota(out, pattern, base, mult, **kw), [], w)

    def relu(qn, out, a, r, w, bias=0.0):
        if qn == "S":
            act(out, a, F.Relu, r, w, bias=bias)
        elif bias:
            ts(out, a, bias, A.add, r, w, 0.0, A.max)
        else:
            ts(out, a, 0.0, A.max, r, w)

    ills = [T.ill0, T.ill1]

    def span(a, b, w=RUN, base=0):
        return slice(base + w * a, base + w * b)

    def slots(buf, a, b, k, first=0, every=1):
        return buf[:, 5 * (RUN * a + first) + k:5 * RUN * b:5 * every]

    whole = {"r": (T.ri, T.res, ["ri"]), "n": (T.ni, T.nb, keys(0, 4, "ni")), "d": (T.dd0, T.dice, [("dd", 0)])}
    for n in LOAD.split():
        if n[0] in whole:
            dma(n[1], whole[n[0]][0][:], whole[n[0]][1][:], [], whole[n[0]][2])
        else:
            a, b = int(n[0]), int(n[1])
            dma(n[2], T.xi[:, span(a, b)], T.x0[:, span(a, b)], [], keys(a, b, "xi"))

    small = dict(allow_small_or_imprecise_dtypes=True)
    iota(T.t2[:], [[-16, 8], [0, 16]], 0, 1, ["t2"])
    iota(T.t1[:], [[-1, 128]], 0, 1, ["t1"])
    fill(T.big[:], 256.0, ["big"])
    mmul(T.ht[:], T.big[:, 0:128], T.big[:, 0:512], True, True, ["big"], [("ht",)])
    fill(T.hi[:, 0:PAD], 0.0, ["pad"])
    fill(T.top[:], 1.0, ["top"])
    fill(T.bp[:], 0.0, ["bp"])
    fill(T.zb[:], 0.0, ["zb"])
    emit("G", lambda: g.affine_select(T.ee[:], T.big[:], [[-1, WIDE], [0, 16]], A.is_equal, 0.0, 0, 1), ["big"], ["ee"])
    ts(T.t2s[:], T.t2[:], 4, A.arith_shift_right, ["t2"], ["t2s"])
    ts(T.su1[:], T.t1[:], 0, A.is_lt, ["t1"], ["su1"], -1.0, A.mult)
    ts(T.mb[:], T.t2s[:], 0, A.is_equal, ["t2s"], ["mb"])
    ts(T.i2[:], T.t1[:], 0, A.is_equal, ["t1"], ["i2"], TOP, A.mult)
    ts(T.idn[:], T.t1[:], 0, A.is_equal, ["t1"], ["idn"])
    ts(T.t3[:], T.t1[:, 0:16], 15, A.bitwise_and, ["t1"], ["t3"])
    tt(T.qq[:], T.su1[:], T.i2[:], A.add, ["su1", "i2"], ["qq"])
    ts(T.r16[:], T.t3[:], 0, A.is_equal, ["t3"], ["r16"], 256.0, A.mult)
    cpy(T.zb[:, 16:24], T.mb[:, 0:128:16], ["mb"], ["zb"])
    cpy(T.bp[:, 16:144:16], T.mb[:, 0:128:16], ["mb"], ["bp"])
    dma("Y", T.er[0:8, :], T.mb[0:128:16, :], ["mb"], ["er"])

    def tally(t, r, a, b):
        o = 80 * (4 * t + r)
        return T.pre[:, o + a:o + b]

    def widen(t, a, b):
        cpy(slots(T.xs, a, b, 4), T.xi[:, span(a, b)], keys(a, b, "xi"), keys(a, b, "x"))

    piece, ebank, turn = {}, {}, [0, 0]

    def total(t, a, b):
        turn[0] = turn[0] + 1 if a else 0
        bank = ("ta", "tb")[turn[0] % 2]
        for r in range(a, b):
            piece[r] = (a, b, turn[0] % 2)
            mmul(T[bank][:, span(r - a, r - a + 1, 8)], slots(T.xs, r, r + 1, 4), T.mb[:, 0:128:16], True, True,
                 ["mb", ("x", r)], [(bank, r - a)])

    def lift(t, a, b):
        turn[1] = turn[1] + 1 if a else 0
        e = ebank[a] = "e%d" % (turn[1] % 2)
        mmul(T[e][:, span(0, b - a)], T.idn[:], slots(T.xs, a, b, 4), True, False, ["idn"] + keys(a, b, "x"), [(e,)])

    def high(t, a, b):
        bank = ("ta", "tb")[piece[a][2]]
        ts(T.hi[:, span(a, b, 8, PAD)], T[bank][:, span(0, b - a, 8)], float(TH), A.is_ge, keys(0, b - a, bank), keys(a, b, "hi"))

    def carry(a, b, par, steps, start, stop):
        bank = ("tb", "ta")[par]
        for d in steps:
            mmul(T[bank][0:8 * (b - a), 64:65], T.hi[:, span(a - d, b - d, 8, PAD)], T.top[:, 0:1], start and d == steps[0],
                 stop and d == steps[-1], ["top", "pad"] + keys(0, b if stop else a, "hi"), [(bank, "c")])

    def within(a, b):
        par = piece[a][2]
        return T.cn[0:8 * (b - a), span(par, par + 1, RUN, 256)], ("cn", "in", par)

    def running(t, a, b):
        carry(a, b, piece[a][2], list(range(1, b - a)), a == 0, True)
        o, k = within(a, b)
        mmul(o, T.hi[:, span(a, b, 8, PAD)], T.qq[:], True, True, ["qq"] + keys(a, b, "hi"), [k])

    def early(t, a, b):
        carry(a, b, 1 - piece[a - 1][2], list(range(b - a, b)), True, False)

    def infected(t, a, b):
        o, k = within(a, b)
        bank = ("tb", "ta")[piece[a][2]]
        ts(T.it[0:8 * (b - a), span(a, a + 1)], o, T[bank][0:8 * (b - a), 64:65], A.subtract, [k, (bank, "c")], [("it", a)],
           TOP - CAP, A.is_gt)

    def quick(t, a, b, j):
        assert a == 0 and RUN * b <= CAP
        o, k = T.cn[0:8 * b, 256:384], ("cn", "in", 0)
        piece[0] = (0, b, 0)
        if j:
            ts(T.it[0:8 * b, 0:RUN], o, float(TH), A.is_ge, [k], [("it", 0)])
            return
        for r in range(b):
            mmul(o, T.zb[:, 16 - 8 * r:16 + 8 * (b - r)], slots(T.xs, r, r + 1, 4), r == 0, r + 1 == b, ["zb", ("x", r)], [k])

    def spread(t, a, b):
        e, (pa, pb, par) = ebank[a], piece[a]
        for r in range(a, b):
            mmul(T[e][:, span(r - a, r - a + 1)], T.ee[0:8 * (pb - pa), span(r - pa, r - pa + 1)],
                 T.it[0:8 * (pb - pa), span(pa, pa + 1)], False, r + 1 == b, ["ee", ("it", pa)], [(e,)])

    def mask(t, a, b, qn):
        e = ebank[a]
        relu(qn, T["win%d" % t][:, span(a, b, RUN, q * P)], T[e][:, span(0, b - a)], [(e,)], keys(a, b, "win", t), -256.0)

    def share(t, a, b):
        send(T["win%d" % t][:, span(a, b, RUN, q * P)], "al%d_%d" % (t, a), keys(a, b, "win", t))

    def counts(t):
        send(tally(t, q, 64, 66), "ac%d" % t, [("pre", t)])

    def listed(t, j):
        ill = ills[t % 2]
        if j == 0:
            for i in range(16):
                mmul(T.cn[:, 128:192], T.bp[:, 16 - i:144 - i], T["win%d" % t][:, q * P + i:(q + 1) * P:16], i == 0, i == 15,
                     ["bp"] + keys(0, 8, "win", t), [("cn", 128)])
        elif j == 1:
            ts(ill[:], T.cn[:, 128:192], float(TH), A.is_ge, [("cn", 128)], [("ill", t % 2)])
            mmul(T.cn[:, 0:64], T.mb[:], ill[:], True, True, ["mb", ("ill", t % 2)], [("cn", 0)])
        else:
            scan(tally(t, q, 1, 68), T.cn[:, 0:67], T.m16[:], 0.0, A.add, A.add, ["m16", ("cn", 0), ("cn", 64)], [("pre", t)])

    def blocks(t, j, qn="V"):
        ill = ills[t % 2]
        o = T.ta[:, 128:132]
        if j == 0:
            for n, l, k, c in ((192, "mq", "mq", "cq"), (256, "lt", "idn", "cd")):
                mmul(T.tb[:, n:n + 64], T[k][:], T[c][:], True, False, [k, c], [("tb", n)])
                mmul(T.tb[:, n:n + 64], T[l][:], ill[:], False, True, [l, ("ill", t % 2)], [("tb", n)])
        elif j == 1:
            tt(T.rl[:], tally(t, q, 0, 64), T.tb[:, 192:256], A.min, [("pre", t), "pre0", ("tb", 192)], ["rl"])
        elif j == 2 and qn == "S":
            act(T.dm[:], T.tb[:, 256:320], F.Copy, [("tb", 256)], ["dm"])
        elif j == 2:
            cpy(T.dm[:], T.tb[:, 256:320], [("tb", 256)], ["dm"])
        elif j == 3:
            if right:
                mmul(o, T.idn[:], tally(t, q, 64, 68), True, False, ["idn", ("pre", t)], [("ta", "r")])
            for i in range(16):
                mmul(o, T.bn[:, 16 - i:144 - i], T.rl[:, i:64:16], i == 0 and not right, i == 15, ["bn", "rl"], [("ta", "r")])
        else:
            ts(T.bo[:], o, float(P * right), A.add, [("ta", "r")], ["bo"])

    def ground(t):
        iota(T.bg[:, 0:P], [[0, P]], 1, 0, ["bg"], **small)

    def spell(t, j):
        if j == 0:
            cpy(T.bg[:].indirect(T.bo[:]), T.dm[:], ["bo", "dm"], ["bg"])
            return
        seg = T["sw%d" % t][:, q * P:(q + 1) * P]
        scan(seg, T.up[:], T.bg[:, 0:P], 1.0, A.add, A.min, [("up", 0), ("up", 4), "bg"], [("sw", t, "own")])

    def tell(t):
        send(T["sw%d" % t][:, q * P:(q + 1) * P], "as%d" % t, [("sw", t, "own")])
        if t < DAYS - 1:
            ground(t)

    def fade(t, a, b, qn):
        relu(qn, slots(T.slot, a, b, 4), slots(T.xs, a, b, 4), keys(a, b, "x"), keys(a, b, "slot", 4), -8.0)

    def places(t, j):
        y = T.sl0[:, 256:512]
        slope, edge, start, gap = (T.ta[:, n:n + 1] for n in range(240, 244))
        if j == 0:
            for o, l, a, b in ((240, "idn", 0, 4), (240, "idk", 4, 8), (243, "idn", 2, 3), (243, "idn", 2, 3)):
                mmul(T.ta[:, o:244], T[l][:], T.cst[:, a:b], a == 0, False, [l, "cst"], [("ta", "k")])
            terms = [(slope, "idk", r) for r in range(4)] + [(gap, "idn", 1), (gap, "idn", 2), (start, "idn", 0), (edge, "idn", 1)]
            for n, (o, l, r) in enumerate(terms):
                mmul(o, T[l][:], tally(t, r, 64, 65), False, n == 7, [l, ("pre", t), ("cnt", t, "rem")], [("ta", "k")])
        elif j == 1:
            ts(y, T["dd%d" % t][:], slope, A.mult, [("dd", t), ("ta", "k")], [("sl0", "y")], start, A.subtract)
        elif j == 2:
            ts(T.hh[:], y, edge, A.is_le, [("sl0", "y"), ("ta", "k")], ["hh"], gap, A.mult)
        elif j == 3:
            tt(T.oi[:], T.hh[:], y, A.subtract, [("sl0", "y"), "hh"], ["oi"])
        else:
            cpy(T["offs%d" % (t % 2)][:], T.oi[:], ["oi"], [("offs", t % 2)])

    def gather(t, a, b, k, qn):
        s = T["win%d" % t][:].indirect(T.off[:, span(a, b, 8, 64 * k)])
        relu(qn, slots(T.slot, a, b, k), s, keys(0, 8, "win", t) + keys(0, 8, "far", t) + [("off", k)], keys(a, b, "slot", k))

    def newx(t, a, b):
        s = span(a, b, 5 * RUN)
        scan(T.xs[:, s], T.step[:, s], T.slot[:, s], 0.0, A.add, A.max,
             keys(0, 5, "step") + [("step", k, o) for k in range(5) for o in (0, 4)] + [n for k in range(5) for n in keys(a, b, "slot", k)], keys(a, b, "x"))

    def result(t, a, b, qn):
        o, x = T.yo[:, span(a, b)], slots(T.xs, a, b, 4)
        if qn == "G":
            emit("G", lambda: g.affine_select(o, x, [[0, RUN * (b - a)]], A.is_equal, 0.0, 0, 0), keys(a, b, "x"), keys(a, b, "yo"))
        else:
            relu(qn, o, x, keys(a, b, "x"), keys(a, b, "yo"))
        dma("Y", T.yx[:, span(a, b)], T.yo[:, span(a, b)], keys(a, b, "yo"), keys(a, b, "yx"))

    def slfetch(t, a, b, qn):
        s = T["sw%d" % t][:].indirect(T["offs%d" % (t % 2)][:, span(a, b, 32)])
        relu(qn, T.rsl[:, span(a, b, 512)], s, [("sw", t, "own"), ("sw", t, "rem"), ("offs", t % 2)], keys(a, b, "rsl"))

    sums = {}

    def opened(t, a, b):
        bank = {0: "ht", 2: "sl1", 3: "sl0"}[a]
        mmul(T[bank][:, span(0, b - a, 64)], T.w2[0:64, :], T.top[0:64, span(0, b - a, 64)], True, False, keys(0, 2, "w2") + ["top"],
             [(bank,)])
        for k in range(a, b):
            sums[k] = (bank, a, b)

    def hits(t, k):
        bank, a, b = sums[k]
        o = T[bank][:, span(k - a, k - a + 1, 64)]
        mmul(o, T.ineg[:], ills[t % 2][:], False, False, ["ineg", ("ill", t % 2)], [(bank,)])
        for i in range(16):
            mmul(o, T.hb[:, 16 - i:144 - i], slots(T.slot, 0, 8, k, i, 16), False, False, ["hb"] + keys(0, 8, "slot", k), [(bank,)])

    def slsum(t, a, b):
        bank, o, end = sums[a]
        for i in range(16):
            mmul(T[bank][:, span(a - o, b - o, 64)], T.cp[:, 16 - i:144 - i], T.rsl[:, P * a + i:P * b:16], False,
                 i == 15 and b == end, ["cp"] + keys(2 * a, 2 * b, "rsl"), [(bank,)])

    def renew(t, a, b):
        s, bank = span(a, b, 64), sums[a][0]
        tt(T.ni[:, s], T.ni[:, s], T[bank][:, span(0, b - a, 64)], A.max, keys(a, b, "ni") + [(bank,)], keys(a, b, "ni"))

    def strip(t, a, b):
        s = span(a, b, 64)
        ts(T.ni[:, s], T.ni[:, s], 4 * P - 1, A.bitwise_and, keys(a, b, "ni"), keys(a, b, "ni"))

    def offnew(t, a, b):
        s = span(a, b, 64)
        cpy(T.off[:, s], T.ni[:, s], keys(a, b, "ni"), keys(a, b, "off"))

    def closed(t, k):
        o = T.ht[:, span(k, k + 1, 64)]
        mmul(o, T.ineg[:], ills[t % 2][:], True, False, ["ineg", ("ill", t % 2)], [("ht", k)])
        for i in range(16):
            mmul(o, T.hb[:, 16 - i:144 - i], slots(T.slot, 0, 8, k, i, 16), False, i == 15, ["hb"] + keys(0, 8, "slot", k), [("ht", k)])

    def struck(t, a, b):
        s = span(a, b, 64)
        act(T.sg[:, s], T.ht[:, s], F.Sign, keys(a, b, "ht"), keys(a, b, "sg"), bias=-512.0 * 4096)
        o = T.cn[:, s]
        mmul(o, T.i2[:], T.top[:, span(0, b - a, 64)], True, False, ["i2", "top"], keys(a, b, "cn", "k"))
        mmul(o, T.i2[:], T.sg[:, s], False, True, ["i2"] + keys(a, b, "sg"), keys(a, b, "cn", "k"))

    def keep(t, a, b):
        s = span(a, b, 64)
        tt(T.no[:, s], T.ni[:, s], T.cn[:, s], A.subtract, keys(a, b, "ni") + keys(a, b, "cn", "k"), keys(a, b, "no"))

    def drawn(t, k):
        bank = ("ta", "tb", "e0", "e1")[k]
        mmul(T[bank][:, 0:64], T.w2[64:96, :], T.top[64:96, 0:64], True, False, [("w2", 2), "top"], [(bank,)])
        mmul(T[bank][:, 0:64], T.i2[:], T.sg[:, span(k, k + 1, 64)], False, False, ["i2", ("sg", k)], [(bank,)])
        sums[k] = (bank, k, k + 1)

    def final(t, k):
        s, bank = span(k, k + 1, 64), sums[k][0]
        tt(T.no[:, s], T.no[:, s], T[bank][:, 0:64], A.max, [("no", k), (bank,)], [("no", k)])

    def store(t, a, b, qn):
        dma(qn, T.ynb[:, span(a, b, 64)], T.no[:, span(a, b, 64)], keys(a, b, "no"), keys(a, b, "ynb"))

    last = T.r16[:, 15:16]

    def number():
        ts(T.rw[:], T.ri[:], -1.0, A.mult, ["ri"], ["rw"])
        dma("Y", T.rneg[0:8, :], T.rw[:], ["rw"], ["rneg"])

    short = [
        lambda: ts(T.pre[:, 80 * q::320], T.top[:, 0:DAYS], 0.0, A.mult, ["top"], ["pre0"]),
        lambda: fill(T.m16[:], -16.0, ["m16"]),
        lambda: fill(T.cn[:, 64:67], 16.0, [("cn", 64)]),
        lambda: ts(T.pmi[:], T.t1[:, 0:1], 15, A.bitwise_and, ["t1"], ["pmi"]),
        lambda: cpy(T.col[:, 0:1], T.pmi[:], ["pmi"], ["col0"]),
        lambda: ts(T.col[:, 1:2], last, (15 + (255.0 - 64 * q) / 256) / 256, A.mult, ["r16", "col0"], ["col1"], T.col[:, 0:1],
                   A.subtract),
        lambda: emit("G", lambda: g.affine_select(T.lt[:], T.mb[:], [[1, 128]], A.is_ge, 0.0, 0, -1), ["mb"], ["lt"]),
        lambda: fill(T.lt[:, 15:128:16], 0.0, ["lt"]),
        lambda: iota(T.cc[:], [[1, 64]], 0, 0, ["cc"], **small),
        lambda: ts(T.cq[:], T.cc[:], -2016.0, A.add, ["cc"], ["cq"], 1.0 / 2048, A.mult),
        lambda: iota(T.csi[:, 0:4], [[2048, 2], [-2048, 2]], 0, 0, [("csi", 0)]),
        lambda: iota(T.csi[:, 4:8], [[-2047, 2], [2047, 2]], 0, 0, [("csi", 1)]),
        lambda: ts(T.cst[:], T.csi[:], 0.5, A.mult, keys(0, 2, "csi"), ["cst"]),
        lambda: fill(T.w2[0:32, :], 255 * 16 / 32, [("w2", 0)]),
        lambda: fill(T.w2[32:64, :], -512 * 4096 / 32, [("w2", 1)]),
        lambda: fill(T.w2[64:96, :], (255 * 16 - 2048) / 32, [("w2", 2)]),
    ]

    def bit(t, a, b):
        short[10 * a + b]()

    def blk():
        act(T.col[:, 2:3], last, F.Copy, ["r16"], ["col2"], scale=-1.0 / 65536)
        act(T.mq[:], T.mb[:], F.Copy, ["mb"], ["mq"], scale=-4096.0)
        act(T.bn[:], T.bp[:], F.Copy, ["bp"], ["bn"], scale=-1.0 / 16)
        act(T.cd[:], T.cc[:], F.Identity, ["cc", "col1", "col2"], ["cd"], scale=T.col[:, 2:3], bias=T.col[:, 1:2])

    def rise():
        act(T.col[:, 3:4], last, F.Copy, ["r16"], ["col3"], scale=-1.0 / 256, bias=1.0)
        for a in (0, 4):
            act(T.up[:, span(a, a + 4)], T.ht[:], F.Identity, [("ht",), "col3"], [("up", a)], scale=0.0, bias=T.col[:, 3:4])

    def resist():
        for n in (0, 1):
            e = "sl%d" % n
            mmul(T[e][:], T.er[:], T.rneg[:, span(n, n + 1, 512)], True, True, ["er", "rneg"], [(e,)])
            act(slots(T.step, 4 * n, 4 * n + 4, 4), T[e][:], F.Copy, [(e,)], [("step", 4, 4 * n)])

    def steps(t, k, qn):
        if qn == "V":
            fill(slots(T.step, 0, 8, k), 0.0 if k else -1024.0, [("step", k)])
        else:
            for a in (0, 4):
                act(slots(T.step, a, a + 4, k), T.ht[:], F.Copy, [("ht",)], [("step", k, a)], scale=0.0, bias=0.0 if k else -1024.0)

    def misc():
        act(T.col[:, 4:5], last, F.Copy, ["r16"], ["col4"], scale=-4097.0 / 256, bias=1.0)
        act(T.ineg[:], T.idn[:], F.Copy, ["idn"], ["ineg"], scale=-2.0 ** 25)
        act(T.hb[:], T.bp[:], F.Copy, ["bp"], ["hb"], scale=4096.0)
        act(T.cp[:], T.bp[:], F.Copy, ["bp", "col4"], ["cp"], scale=T.col[:, 4:5])
        act(T.idk[:], T.idn[:], F.Copy, ["idn"], ["idk"], scale=1.0 / 2048)

    def draws(t, n):
        ts(T["dd%d" % n][:], T.dd0[:], STEP * n, A.add, [("dd", 0)], [("dd", n)])

    def wrap(t, n):
        ts(T["dd%d" % n][:], T["dd%d" % n][:], M2, A.bitwise_and, [("dd", n)], [("dd", n)])

    once = {"num": number, "blk": blk, "rise": rise, "res": resist, "misc": misc}
    flags = {"x": widen, "T": total, "l": lift, "a": high, "F": running, "E": early, "i": infected, "s": spread, "m": mask,
             "W": share, "C": counts, "N": tell, "L": listed, "Z": blocks, "M": spell, "D": fade, "B": ground, "q": quick}
    day = {"g": gather, "c": newx, "y": result, "k": slfetch, "S": slsum, "H": opened, "A": strip, "R": renew, "O": offnew,
           "h": hits, "p": places, "d": draws, "w": wrap, "z": steps, "b": bit,
           "j": closed, "u": struck, "K": keep, "J": drawn, "r": final, "o": store}

    def run(t, order):
        for n in order.split():
            a = [int(c) if c.isdigit() else c for c in n[1:]]
            if n in once:
                once[n]()
            elif n[0] in flags:
                flags[n[0]](t + 1, *a)
            else:
                day[n[0]](t, *a)

    for t, order in enumerate((FIRST, DAY, DAY, DAY, LAST)):
        run(t - 1, order)

    sync_to("G", [lastw[k] for k in keys(0, 4, "ynb") + keys(0, 8, "yx")])
    for k in ("V", "S", "P", "G"):
        g.wait_ge(T.sem[psem[k]], done[k])
    g.wait_ge(T.sem.sent, nsent[0])
